import numpy as np, ml_dtypes
CORES = [35,38,43,46]
N = 4
import mx_ref
BF = ml_dtypes.bfloat16
def gentries(a):
    return np.ascontiguousarray(a.reshape(8, 16, -1).transpose(0, 2, 1)).reshape(8, -1)
def gtable(e):
    e = np.asarray(e); return np.ascontiguousarray(e.reshape(8, -1, 16).transpose(0, 2, 1)).reshape(128, -1).astype(np.int32)
def gcols(t, e):
    v = np.concatenate([t.reshape(8, 16, -1, 4), np.zeros((8, 16, 1, 4), BF)], axis=2)
    return np.ascontiguousarray(np.stack([v[g][:, e[g]] for g in range(8)])).reshape(128, -1)
def tile(rs):
    return np.stack(rs, axis=2).reshape(128, -1).astype(BF)
def pick(q, e):
    c = np.concatenate([q[0].reshape(128, -1, 4), np.zeros((128, 1, 4), np.uint8)], axis=1); s = np.concatenate([q[1], np.ones((16, 1), np.uint8)], axis=1)
    return (np.ascontiguousarray(c[:, e].reshape(128, -1)), np.ascontiguousarray(s[:, e]))
def join(*qs):
    return (np.concatenate([q[0] for q in qs], axis=1), np.concatenate([q[1] for q in qs], axis=1))
def put(q, e, v):
    c, s = q[0].reshape(128, -1, 4).copy(), q[1].copy(); c[:, e] = v[0].reshape(128, -1, 4); s[:, e] = v[1]
    return (c.reshape(128, -1), s)
def pk(c, s):
    return (np.ascontiguousarray(c), mx_ref.live(s))
def emit(q):
    return q[0], q[1]
def packed(v, rng):
    q = [mx_ref.quantize(np.ascontiguousarray(v[r])) for r in range(N)]
    return np.stack([a for a, b in q]), np.stack([mx_ref.plane(b, rng) for a, b in q])
def values_of_codes():
    e, c = np.zeros((128, 128, 4), np.float32), np.zeros((128, 2, 4), np.uint8)
    e[np.arange(128), np.arange(128), 0] = 1
    c[:127, :, 0] = np.arange(256).reshape(2, 128).T[:127]
    return mx_ref.matmul(mx_ref.quantize(e.reshape(128, 512).astype(BF)), (c.reshape(128, 8), np.full((16, 2), 127, np.uint8))).T.reshape(-1).astype(np.float64)
CODE_VALUE, SCALE_VALUE = values_of_codes(), 2.0 ** (np.arange(256) - 127.0)
def decode(q):
    return (CODE_VALUE[q[0]].reshape(16, 8, -1, 4) * SCALE_VALUE[q[1]][:, None, :, None] + 0.0).reshape(128, -1).astype(np.float32)
def f(rng, *shape):
    return mx_ref.flush((rng.standard_normal(shape, dtype=np.float32) * np.exp2(rng.integers(-2, 3, shape[:-1] + (1,)))).astype(BF))
def wide(rng, *shape, cols=0):
    v = rng.standard_normal(shape, dtype=np.float32) * np.exp2(rng.integers(-12, 13, shape)).astype(np.float32)
    if cols: v *= np.repeat(np.exp2(rng.integers(-cols, cols + 1, shape[:-2] + (1, shape[-1] // 4))) * (rng.random(shape[:-2] + (1, shape[-1] // 4)) > 0.0625), 4, axis=-1).astype(np.float32)
    return mx_ref.flush(v.astype(BF))
C, H = 384, 192
MASK = [1, 2, 3]
def numbers_of(rng):
    return {"x": np.array(f(rng, N, 128, 4 * C)), "u": np.array(f(rng, N, 128, 512)), "v": np.array(f(rng, N, 128, 512))}
def stored(l, k):
    return {"gl": np.stack([gtable(l[r]) for r in range(N)]), "gk": np.stack([gtable(k[r]) for r in range(N)])}
def lists(rng):
    e = np.tile(np.arange(C), (N, 8, 1))
    return stored(rng.permuted(e, axis=2), rng.permuted(e, axis=2))
def layers(rng, still=[]):
    w = np.array(f(rng, N, 128, 2048)).reshape(N, 8, 16, 4, 8, 16, 4)
    for i in still:
        w[:, :, i] = 0
        w[:, :, :, :, :, i] = 0
    return w
def weights(rng, w):
    c, p = packed(np.ascontiguousarray(w).reshape(N, 128, 2048), rng)
    return {"wc": c, "ws": p}
def setup_inputs(rng):
    return {**numbers_of(rng), **lists(rng), **weights(rng, layers(rng))}
def setup_inputs_ties(rng):
    d = numbers_of(rng)
    o = rng.permutation(N)
    k = rng.integers(-1, 2, (N, 8, C, 2)).astype(np.float32)
    k[o[1]] = 1
    k[o[2]] = -1
    x = d["x"].reshape(N, 8, 16, C, 4)
    x[:, :, 0] = 0
    x[:, :, 0, :, :2] = k.astype(BF)
    a = np.exp2(rng.integers(-3, 4, 8).astype(np.float32))[None, :, None]
    x[:, :, 8:] = 0
    x[:, :, 8, :, 0] = (-1.125 * a).astype(BF)
    x[:, :, 10, :, 0] = (-0.0703125 * a).astype(BF)
    c = np.ones(N, np.float32)
    c[o[0]] = 0
    u = d["u"].reshape(N, 128, 128, 4)
    for t in range(2):
        u[:, :, t::16] = 0
        for h in range(0, 128, 16): u[:, h, h + t, t] = c.astype(BF)
    w = layers(rng, [0])
    w[:, :, :, :, :, 8:] = 0
    for g in range(8):
        w[:, g, 8, 0, g, 8, 0] = -28.0
        for b in range(4): w[:, g, 10, b, g, 9, 0] = -2.0 ** (b - 5)
    return {"x": x.reshape(N, 128, 4 * C), "u": u.reshape(N, 128, 512), "v": d["v"], **stored(rng.integers(0, C, (N, 8, C)), rng.integers(0, C, (N, 8, C))), **weights(rng, w)}
def setup_inputs_near(rng):
    d = numbers_of(rng)
    o = rng.permutation(N) % 2
    k = np.where(o == 0, 2.0 ** -30, 1.0).astype(np.float32)
    x = d["x"].astype(np.float32).reshape(N, 8, 16, C, 4)
    x[:, :, :8] = 0
    s = rng.integers(-1, 2, (N, 8, C, 2)) * k[:, None, None, None]
    x[:, :, 0, :, :2] = 1.125 * s
    x[:, :, 1, :, :2] = -1.25 * s
    x[:, :, 3, :, :2] = rng.choice([-1.0, 1.0], (N, 8, C, 2)) * 2.0 ** -30
    x[:, :, 5] = 2.0 ** -30
    for r in range(N):
        for g in rng.permutation(8)[:4]: x[r, g, 0, rng.integers(C), 0] = 2.0 ** 30 * rng.choice([-1.0, 1.0])
    u = d["u"].reshape(N, 128, 128, 4)
    w = layers(rng, range(8))
    for t in range(2):
        u[:, :, t::16] = 0
        for h in range(0, 128, 16):
            u[:, h, h + t, t] = (1.125 * k).astype(BF)
            u[:, h + 1, h + t, t] = k.astype(BF)
            u[:, h + 2, h + t, t] = k.astype(BF)
        for g in range(8):
            w[:, g, 3, t, g, 2, t] = 2.0 ** -8
            w[:, g, 3, t, g, 4, t] = 32.0
    return {"x": x.reshape(N, 128, 4 * C).astype(BF), "u": u.reshape(N, 128, 512), "v": d["v"], **lists(rng), **weights(rng, w)}
def setup_inputs_odd(rng):
    d = numbers_of(rng)
    x = (1.0 + (2 * rng.integers(0, 64, (N, 16, 8, C, 4)) + 1) * 2.0 ** -7) * np.exp2(-rng.integers(0, 7, (N, 16, 8, C, 4)).astype(np.float64)) * rng.choice([-1.0, 1.0], (N, 16, 8, C, 4))
    x[:, :, 0, :, 0] = 1.96875 * 2.0 ** 8 * rng.choice([-1.0, 1.0], (N, 16, C))
    x[:, ::2, 1, :, :2] = rng.integers(7, 10, (N, 8, C, 2)) * 2.0 ** -8
    x[:, ::2, 2, :, :2] = 2.0 ** -5
    u = d["u"].reshape(N, 16, 8, 128, 4)
    for t in range(2):
        u[:, :, :, t::16] = 0
        for g in range(8):
            u[:, 2 * g, 1, 16 * g + t, t] = 1.0
            u[:, 2 * g, 2, 16 * g + t, t] = -1.0
    return {"x": x.astype(np.float32).reshape(N, 128, 4 * C).astype(BF), "u": u.reshape(N, 128, 512), "v": d["v"], **lists(rng), **weights(rng, layers(rng, [0, 1, 2, 8]))}
def setup_inputs_ends(rng):
    d = numbers_of(rng)
    x = np.zeros((N, 128, C, 4))
    u = d["u"].astype(np.float32).reshape(N, 128, 128, 4)
    v = d["v"].astype(np.float32)
    w = np.zeros((N, 128, 4, 128, 4), np.float32)
    o, e = rng.permutation(N) % 4, rng.permutation(N) % 4
    i = np.arange(128)
    def amount(large, *n):
        return (0.9 + 0.1 * rng.random(n)) * 2.0 ** 30 if large else (1.0 + 0.125 * rng.integers(0, 8, n)) * 2.0 ** -30
    for r in range(N):
        large = o[r] < 2
        if o[r] == 3: x[r] = d["x"][r].astype(np.float32).reshape(128, C, 4)[:, :1]
        else: x[r] = -amount(large, 128, C, 4) * (0.5 if large else 1.0)
        if o[r] == 1: x[r] *= rng.choice([-1.0, 1.0], (1, C, 1))
        x[r, 7::8] = 2.0 ** -30
        for t in range(2):
            h = rng.permutation(8)
            c = np.where(h < 2, 0.0, h % 2 * 2.0 - 1.0)[None, :, None]
            if o[r] == 3: u[r, :, t::16] *= np.abs(c).astype(np.float32)
            else: u[r, :, t::16] = c * amount(large, 128, 8, 4)
        v[r] = rng.choice([-1.0, 1.0], (128, 512)) * amount(large, 128, 512)
        k = np.array([1.0, 2.0, 4.0])[rng.permutation(8) % 3][i // 16]
        k[7::8] = 0
        if o[r] == 2: k = np.where(i % 8 == 7, 2.0 ** 8, 2.0 ** -8)
        for b in range(4): w[r, i, b, i, b] = k
    both = []
    for z in (e, (e + rng.integers(1, 4)) % 4):
        a = rng.integers(0, C, (N, 8, C))
        a[z == 0] = C - 1
        a[z == 1] = 0
        a[z == 2] = rng.integers(0, 2, a[z == 2].shape) * (C - 1)
        both.append(a)
    return {"x": x.astype(np.float32).reshape(N, 128, 4 * C).astype(BF), "u": u.reshape(N, 128, 512).astype(BF), "v": v.astype(BF), **stored(*both), **weights(rng, w.astype(BF))}
def setup_inputs_spread(rng):
    d = setup_inputs(rng)
    d["x"] = wide(rng, N, 128, 4 * C, cols=6)
    return d
def check_inputs(d):
    b = []
    for k in ("x", "u", "v"):
        a = np.abs(d[k].astype(np.float32))
        if not (np.isfinite(a).all() and ((a == 0) | (a >= 2.0 ** -30) & (a <= 2.0 ** 30)).all()): b.append("a value of " + k)
    for k in ("gl", "gk"):
        if not ((d[k] >= 0) & (d[k] < C)).all(): b.append("an entry of " + k)
    none, least, most = [emit(mx_ref.quantize(np.full((128, 16), k, np.float32).astype(BF)))[1][0, 0] for k in (0.0, 2.0 ** -8, 2.0 ** 8)]
    for r in range(N):
        if ((d["wc"][r] == 0x7F) | (d["wc"][r] == 0xFF)).any(): b.append("wc: a code that is no number")
        s = mx_ref.live(d["ws"][r])
        if ((s != none) & ((s < least) | (s > most))).any(): b.append("ws: a scale out of range")
        if (((d["wc"][r].reshape(16, 8, 512, 4) & 0x7F) != 0) & (s == none)[:, None, :, None]).any(): b.append("wc: a code other than zero under the scale of zeros")
    return b
def at(t, e):
    return np.take_along_axis(t, e, axis=1)
def reference(x, u, v, gl, gk, wc, ws):
    qu = [mx_ref.quantize(u[r]) for r in range(N)]
    lay = [pk(wc[r], ws[r]) for r in range(N)]
    left, right = [gentries(gl[r]) for r in range(N)], [gentries(gk[r]) for r in range(N)]
    now = [x[r] for r in range(N)]
    for mask in MASK:
        point, made, sent, turn = [], [], [], []
        for r in range(N):
            l, k = left[r], right[r]
            s = mx_ref.matmul(qu[r], mx_ref.quantize(now[r]))
            b = s[::16] > 0
            turn.append(s[1::16][:, :H] < 0)
            state, down = b, []
            for t in range(3):
                a, c = at(state, l), at(state, k)
                down.append(np.where(a, l, np.where(c, k, np.arange(C))))
                state = b ^ (a & ~c)
            o = at(down[0], at(down[1], down[2]))
            z = (gcols(now[r], o).astype(np.float32) + gcols(now[r], at(l, o)).astype(np.float32)) * np.float32(0.5)
            q = mx_ref.quantize(z.astype(BF))
            h = tile([mx_ref.matmul(pick(lay[r], np.arange(128 * b, 128 * b + 128)), q) * np.float32(0.03125) for b in range(4)])
            point.append(o)
            made.append(h)
            sent.append(decode(mx_ref.quantize(h)).astype(BF))
        for r in range(N):
            p = r ^ mask
            l, k = left[r], right[r]
            m = at(point[p], k)
            add = np.concatenate([gcols(sent[p], m[:, :H]), gcols(made[r], m[:, H:])], axis=1)
            now[r] = (now[r].astype(np.float32) + add.astype(np.float32)).astype(BF)
            t = np.concatenate([turn[r], turn[r]], axis=1)
            left[r] = np.where(t, np.roll(k, H, axis=1), l)
            right[r] = np.where(t, np.roll(l, H, axis=1), k)
    y, lr = np.zeros((N, 128, C), np.float32), np.zeros((N, 8, 2 * C), np.float32)
    oc, osc = np.zeros((N, 128, 4 * C), np.uint8), np.zeros((N, 16, C), np.uint8)
    for r in range(N):
        q = mx_ref.quantize(now[r])
        y[r] = mx_ref.matmul(mx_ref.quantize(v[r]), q)
        lr[r] = np.concatenate([left[r], right[r]], axis=1)
        oc[r], osc[r] = emit(q)
    return {"y": y, "lr": lr, "oc": oc, "osc": osc}

@@ -1,0 +1,502 @@
+from concourse.bass import DstId, RemoteDMATransfer
+from concourse.mybir import dt, AluOpType, ActivationFunctionType
+
+OP = AluOpType
+AF = ActivationFunctionType
+C, HC, K24, K12 = 384, 192, 24, 12
+MASK = [1, 2, 3]
+ROUNDS = 3
+EARLY = False
+WGT = 256.0
+
+SCRATCH = {
+    "x0": ("sbuf", [128, 4 * C], "bfloat16"),
+    "x1": ("sbuf", [128, 4 * C], "bfloat16"),
+    "x2": ("sbuf", [128, 4 * C], "bfloat16"),
+    "x3": ("sbuf", [128, 4 * C], "bfloat16"),
+    "xq": ("sbuf", [128, C], "float8_e4m3fn_x4"),
+    "xs": ("sbuf", [128, C], "uint8"),
+    "pp": ("sbuf", [128, 4 * C], "bfloat16"),
+    "zt": ("sbuf", [128, 4 * C], "bfloat16"),
+    "zq": ("sbuf", [128, C], "float8_e4m3fn_x4"),
+    "zs": ("sbuf", [128, C], "uint8"),
+    "h0": ("sbuf", [128, C], "bfloat16"),
+    "h1": ("sbuf", [128, C], "bfloat16"),
+    "h2": ("sbuf", [128, C], "bfloat16"),
+    "h3": ("sbuf", [128, C], "bfloat16"),
+    "ht": ("sbuf", [128, 4 * HC], "bfloat16"),
+    "hq": ("sbuf", [128, HC], "float8_e4m3fn_x4"),
+    "hs": ("sbuf", [128, HC], "uint8"),
+    "ut": ("sbuf", [128, 512], "bfloat16"),
+    "uq": ("sbuf", [128, 128], "float8_e4m3fn_x4"),
+    "us": ("sbuf", [128, 128], "uint8"),
+    "uq2": ("sbuf", [128, 256], "float8_e4m3fn_x4"),
+    "us2": ("sbuf", [128, 256], "uint8"),
+    "vt": ("sbuf", [128, 512], "bfloat16"),
+    "vq": ("sbuf", [128, 128], "float8_e4m3fn_x4"),
+    "vs": ("sbuf", [128, 128], "uint8"),
+    "wq": ("sbuf", [128, 512], "float8_e4m3fn_x4"),
+    "wp": ("sbuf", [128, 512], "uint8"),
+    "one": ("sbuf", [128, 128], "bfloat16"),
+    "eye": ("sbuf", [128, 128], "bfloat16"),
+    "et": ("sbuf", [128, 2048], "bfloat16"),
+    "eq": ("sbuf", [128, 512], "float8_e4m3fn_x4"),
+    "es": ("sbuf", [128, 512], "uint8"),
+    "ulist": ("sbuf", [128, 16], "int32"),
+    "ulist16": ("sbuf", [128, 16], "uint16"),
+    "ddi": ("sbuf", [128, 16], "int32"),
+    "ddm": ("sbuf", [128, 16], "int32"),
+    "wga": ("sbuf", [128, 16], "bfloat16"),
+    "wgb": ("sbuf", [128, 16], "bfloat16"),
+    "wgt": ("sbuf", [128, 768], "bfloat16"),
+    "sel": ("sbuf", [128, C], "float32"),
+    "jj": ("sbuf", [128, C], "float32"),
+    "rst": ("sbuf", [128, C], "float32"),
+    "nat": ("sbuf", [128, C], "float32"),
+    "pi": ("sbuf", [128, K24], "int32"),
+    "pm": ("sbuf", [128, K24], "int32"),
+    "q16": ("sbuf", [128, K24], "int32"),
+    "cw": ("sbuf", [128, K24], "float32"),
+    "last": ("sbuf", [128, 4], "float32"),
+    "fac": ("sbuf", [128, 4], "float32"),
+    "gin": ("sbuf", [128, 2 * K24], "int32"),
+    "lk0": ("sbuf", [128, 2 * K24], "float32"),
+    "lk1": ("sbuf", [128, 2 * K24], "float32"),
+    "lk2": ("sbuf", [128, 2 * K24], "float32"),
+    "lk3": ("sbuf", [128, 2 * K24], "float32"),
+    "lu0": ("sbuf", [128, 2 * K24], "uint16"),
+    "lu1": ("sbuf", [128, 2 * K24], "uint16"),
+    "lu2": ("sbuf", [128, 2 * K24], "uint16"),
+    "lu3": ("sbuf", [128, 2 * K24], "uint16"),
+    "la0": ("sbuf", [128, K24], "uint16"),
+    "la1": ("sbuf", [128, K24], "uint16"),
+    "la2": ("sbuf", [128, K24], "uint16"),
+    "la3": ("sbuf", [128, K24], "uint16"),
+    "pr": ("sbuf", [128, 4 * K24], "float32"),
+    "kk": ("sbuf", [128, 2 * K24], "float32"),
+    "dif": ("sbuf", [128, K24], "float32"),
+    "tt": ("sbuf", [128, K24], "float32"),
+    "ud": ("sbuf", [128, K24], "float32"),
+    "b": ("sbuf", [128, C], "bfloat16"),
+    "ga": ("sbuf", [128, C], "bfloat16"),
+    "tx": ("sbuf", [128, 768], "bfloat16"),
+    "c0": ("sbuf", [128, C], "bfloat16"),
+    "c3": ("sbuf", [128, C], "bfloat16"),
+    "c1": ("sbuf", [128, C], "bfloat16"),
+    "yy": ("sbuf", [128, C], "bfloat16"),
+    "gb": ("sbuf", [128, C], "bfloat16"),
+    "xx": ("sbuf", [128, C], "bfloat16"),
+    "raw": ("sbuf", [128, 768], "bfloat16"),
+    "raw2": ("sbuf", [128, C], "bfloat16"),
+    "xi": ("sbuf", [128, 2 * K24], "int32"),
+    "sq": ("sbuf", [128, 2 * K24], "float32"),
+    "mm": ("sbuf", [128, 4 * K24], "float32"),
+    "mp": ("sbuf", [128, 4 * K24], "float32"),
+    "ms": ("sbuf", [128, 2 * K24], "float32"),
+    "d01": ("sbuf", [128, 2 * K24], "uint16"),
+    "xj": ("sbuf", [128, K24], "int32"),
+    "xd": ("sbuf", [128, K24], "float32"),
+    "sq2": ("sbuf", [128, K24], "float32"),
+    "mm2": ("sbuf", [128, 2 * K24], "float32"),
+    "mp2": ("sbuf", [128, 2 * K24], "float32"),
+    "ms2": ("sbuf", [128, K24], "float32"),
+    "d2": ("sbuf", [128, K24], "uint16"),
+    "dn": ("sbuf", [128, C], "float32"),
+    "qn": ("sbuf", [128, C], "float32"),
+    "on": ("sbuf", [128, C], "float32"),
+    "om": ("sbuf", [128, C], "float32"),
+    "ow": ("sbuf", [128, C], "float32"),
+    "of0": ("sbuf", [128, K24], "uint16"),
+    "of1": ("sbuf", [128, K24], "uint16"),
+    "of2": ("sbuf", [128, K24], "uint16"),
+    "of3": ("sbuf", [128, K24], "uint16"),
+    "mn": ("sbuf", [128, C], "float32"),
+    "mw": ("sbuf", [128, C], "float32"),
+    "mu": ("sbuf", [128, K24], "uint16"),
+    "ts": ("sbuf", [128, HC], "bfloat16"),
+    "tw": ("sbuf", [128, HC], "bfloat16"),
+    "kin1": ("sbuf", [128, K24], "uint16"),
+    "kin2": ("sbuf", [128, K24], "uint16"),
+    "kin3": ("sbuf", [128, K24], "uint16"),
+    "min1": ("sbuf", [128, K12], "uint16"),
+    "min2": ("sbuf", [128, K12], "uint16"),
+    "min3": ("sbuf", [128, K12], "uint16"),
+    "dq1": ("sbuf", [128, HC], "float8_e4m3fn_x4"),
+    "dq2": ("sbuf", [128, HC], "float8_e4m3fn_x4"),
+    "dq3": ("sbuf", [128, HC], "float8_e4m3fn_x4"),
+    "ds1": ("sbuf", [128, HC], "uint8"),
+    "ds2": ("sbuf", [128, HC], "uint8"),
+    "ds3": ("sbuf", [128, HC], "uint8"),
+    "yo": ("sbuf", [128, C], "float32"),
+    "lro": ("sbuf", [128, 2 * C], "float32"),
+    "ps0": ("psum", [128, 512], "float32"),
+    "ps1": ("psum", [128, 512], "float32"),
+    "ps2": ("psum", [128, 512], "float32"),
+    "ps3": ("psum", [128, 512], "float32"),
+    "ps4": ("psum", [128, 512], "float32"),
+    "ps5": ("psum", [128, 512], "float32"),
+    "ps6": ("psum", [128, 512], "float32"),
+    "ps7": ("psum", [128, 512], "float32"),
+}
+SEMAPHORES = ["cv", "cs", "ct", "cg"]
+SEMAPHORES += ["i%d" % i for i in range(10)]
+SEMAPHORES += ["pa%d_%d" % (r, h) for r in (1, 2, 3) for h in (0, 1)]
+SEMAPHORES += [n + "%d" % r for r in (1, 2, 3) for n in ("rk", "rm", "rc", "rs", "lk", "lm", "lc", "ls")]
+SEMAPHORES += ["o%d" % i for i in range(24)]
+
+COMPUTE = {"v": "cv", "s": "cs", "t": "ct", "g": "cg"}
+
+
+def rank_program(g, core, T, topo):
+    rank = T.rank_of(core)
+    if rank is None:
+        return
+    queue = {"v": g.vector, "s": g.scalar, "t": g.tensor, "y": g.sync, "g": g}
+    total = {}
+    known = {q: {} for q in queue}
+    seen = {}
+
+    def A(name, lo=0, hi=None, step=1):
+        t = T[name]
+        n = t.shape[1]
+        hi = n if hi is None else hi
+        ap = t[:, lo:hi] if step == 1 else t[:, lo:hi:step]
+        return (ap, [(name, lo, hi, step)])
+
+    def U8(name, lo, hi):
+        return (T[name][:, lo:hi].bitcast(dt.uint8), [(name, lo, hi, 1)])
+
+    def IND(win, off, a, b):
+        n = T[win].shape[1]
+        return (T[win][:, 0:n].indirect(T[off][:, a:b]), [(win, 0, n, 1), (off, a, b, 1)])
+
+    def clash(p, q):
+        if p[0] >= q[1] or q[0] >= p[1]:
+            return False
+        return not (p[2] == 4 and q[2] == 4 and (p[0] - q[0]) % 4)
+
+    def learn(q, sem, val, clock):
+        k = known[q]
+        k[sem] = max(k.get(sem, 0), val)
+        for s, v in clock.items():
+            if v > k.get(s, 0):
+                k[s] = v
+
+    def order(q, reads, writes):
+        need = []
+        for w, regs in ((False, reads), (True, writes)):
+            for name, lo, hi, step in regs:
+                bank = name[:2] == "ps"
+                for (reg, rw, rq, sem, val, clock, slow) in seen.get(name, ()):
+                    if not (w or rw or (bank and rq != q)):
+                        continue
+                    if rq == q and not slow and not rw:
+                        continue
+                    if bank or clash(reg, (lo, hi, step)):
+                        if known[q].get(sem, 0) < val:
+                            need.append((val, sem, clock))
+        best = {}
+        for val, sem, clock in need:
+            if sem not in best or best[sem][0] < val:
+                best[sem] = (val, clock)
+        todo = []
+        for sem, (val, clock) in best.items():
+            if not any(s2 != sem and c2.get(sem, 0) >= val for s2, (v2, c2) in best.items()):
+                todo.append((sem, val, clock))
+        for sem, val, clock in todo:
+            queue[q].wait_ge(T.sem[sem], val)
+            learn(q, sem, val, clock)
+
+    def note(q, reads, writes, sem, val, clock, slow):
+        for w, regs in ((False, reads), (True, writes)):
+            for name, lo, hi, step in regs:
+                seen.setdefault(name, []).append(((lo, hi, step), w, q, sem, val, clock, slow))
+
+    def op(q, call, outs, ins):
+        reads = [r for _, regs in ins for r in regs]
+        writes = [r for _, regs in outs for r in regs]
+        order(q, reads, writes)
+        sem = COMPUTE[q]
+        total[sem] = total.get(sem, 0) + 1
+        call().then_inc(T.sem[sem], 1)
+        note(q, reads, writes, sem, total[sem], dict(known[q]), False)
+
+    def load(q, out, in_, sem, **kw):
+        order(q, in_[1], out[1])
+        total[sem] = total.get(sem, 0) + 16
+        queue[q].dma_start(out[0], in_[0], **kw).then_inc(T.sem[sem], 16)
+        note(q, in_[1], out[1], sem, total[sem], dict(known[q]), True)
+
+    def X(ap):
+        return (ap, [])
+
+    def send(out, in_, dst, rsem, lsem):
+        order("g", in_[1], [])
+        rid, pid = topo.addr(dst)[:2]
+        n = len(topo.engines(core, dst))
+        g.remote_dma(out_ap=out[0], in_ap=in_[0], remote_sem=T.sem[rsem], local_sem=T.sem[lsem],
+                     pid=pid, routing_id=rid, dma_engine_mask=topo.mask(core, dst))
+        total[lsem] = total.get(lsem, 0) + n
+        note("g", in_[1], [], lsem, total[lsem], dict(known["g"]), True)
+        total[rsem] = total.get(rsem, 0) + len(topo.engines(dst, core))
+        note("far", [], out[1], rsem, total[rsem], {}, True)
+
+    def ts(out, a, s1, o1, s2=None, o2=None):
+        k1 = s1[0] if isinstance(s1, tuple) else s1
+        ins = [a] + ([s1] if isinstance(s1, tuple) else [])
+        if o2 is None:
+            op("v", lambda: g.vector.tensor_scalar(out[0], a[0], k1, None, o1), [out], ins)
+        else:
+            op("v", lambda: g.vector.tensor_scalar(out[0], a[0], k1, s2, o1, o2), [out], ins)
+
+    def tt(out, a, b, o):
+        op("v", lambda: g.vector.tensor_tensor(out[0], a[0], b[0], o), [out], [a, b])
+
+    def vcopy(out, a):
+        op("v", lambda: g.vector.tensor_copy(out[0], a[0]), [out], [a])
+
+    def act(out, a, func=AF.Copy, scale=1.0, bias=0.0):
+        more = {k: v for k, v, d in (("bias", bias, 0.0), ("scale", scale, 1.0)) if v != d}
+        op("s", lambda: g.scalar.activation(out[0], a[0], func, **more), [out], [a])
+
+    def scan(out, d0, d1):
+        op("v", lambda: g.vector.tensor_tensor_scan(out[0], d0[0], d1[0], 0.0, OP.mult, OP.add), [out], [d0, d1])
+
+    def quant(code, plane, a):
+        op("v", lambda: g.vector.quantize_mx(code[0], plane[0], a[0]), [code, plane], [a])
+
+    def mm(bank, lhs, lhs_s, a, rhs, rhs_s, lo, hi):
+        out, w, ws_ = A(bank, 0, hi - lo), A(lhs, a, a + 128), A(lhs_s, a, a + 128)
+        x, xs_ = A(rhs, lo, hi), A(rhs_s, lo, hi)
+        op("t", lambda: g.tensor.matmul_mx(out[0], w[0], ws_[0], x[0], xs_[0], True, True), [out], [w, ws_, x, xs_])
+
+    def iota(out, pattern, cm, base=0, small=False):
+        if small:
+            op("g", lambda: g.iota(out[0], pattern, base, cm, allow_small_or_imprecise_dtypes=True), [out], [])
+        else:
+            op("g", lambda: g.iota(out[0], pattern, base, cm), [out], [])
+
+    VIEW48, VIEW24, VIEW12 = (15, 768, 16), (15, C, 16), (15, HC, 16)
+
+    load("y", A("ut"), X(T.u[:]), "i0")
+    load("s", A("gin", K24, 2 * K24), X(T.gk[:]), "i1")
+    load("y", A("x0"), X(T.x[:]), "i2")
+    iota(A("ulist"), [[1, 2], [16, 8]], 0)
+    iota(A("ddi"), [[1, 16]], -1, base=128)
+    iota(A("pi"), [[0, K24]], 1)
+    iota(A("q16"), [[16, K24]], 0)
+    load("g", A("gin", 0, K24), X(T.gl[:]), "i3")
+    load("y", U8("wq", 0, 512), X(T.wc[:]), "i4")
+    load("y", A("wp"), X(T.ws[:]), "i5")
+    load("y", A("vt"), X(T.v[:]), "i6")
+
+    vcopy(A("ulist16"), A("ulist"))
+    ts(A("ddm"), A("ddi"), 15, OP.bitwise_and)
+    ts(A("wga"), A("ddm"), 1, OP.is_equal, WGT - 1.0, OP.mult)
+    ts(A("wgb"), A("ddm"), 0, OP.not_equal)
+    tt(A("wgt", 0, 16), A("wga"), A("wgb"), OP.add)
+    ts(A("sel", 0, 16), A("ddm"), 0, OP.is_equal)
+    ts(A("pm"), A("pi"), 15, OP.bitwise_and)
+    tt(A("cw"), A("pm"), A("q16"), OP.add)
+    ts(A("last", 0, 1), A("pm", 0, 1), 15, OP.is_equal)
+    ts(A("fac", 0, 1), A("last", 0, 1), 1.0 - 1.0 / WGT, OP.mult, 1.0 / WGT, OP.add)
+    op("v", lambda: g.vector.memset(T.one[:], 1.0), [A("one")], [])
+    op("v", lambda: g.vector.memset(T.et[:], 0.0), [A("et")], [])
+    for name, width in (("wgt", 768), ("sel", C)):
+        have = 16
+        while have < width:
+            more = min(have, width - have)
+            act(A(name, have, have + more), A(name, 0, more))
+            have += more
+    vcopy(A("lu0", K24, 2 * K24), A("gin", K24, 2 * K24))
+
+    def partner(r):
+        return T.cores[rank ^ MASK[r - 1]]
+
+    def send_children(r):
+        send(A("kin%d" % r), A("lu%d" % (r - 1), K24, 2 * K24), partner(r), "rk%d" % r, "lk%d" % r)
+
+    def lists_of(n, first):
+        L = "lk%d" % n
+        if first:
+            vcopy(A("lu%d" % n, 0, K24), A("gin", 0, K24))
+            vcopy(A(L), A("gin"))
+        else:
+            vcopy(A("lu%d" % n), A(L))
+        for t in range(4):
+            ts(A("la%d" % t), A(L, 0, K24), 4.0, OP.mult, float(t), OP.add)
+
+    def pairs_of(n):
+        L = "lk%d" % n
+        tt(A("pr", K24, 2 * K24), A(L, 0, K24), A(L, K24, 2 * K24), OP.subtract)
+        tt(A("pr", 2 * K24, 3 * K24), A("cw"), A(L, K24, 2 * K24), OP.subtract)
+        tt(A("dif", 0, K12), A(L, 3 * K12, 4 * K12), A(L, 0, K12), OP.subtract)
+        tt(A("dif", K12, K24), A(L, 2 * K12, 3 * K12), A(L, K12, 2 * K12), OP.subtract)
+
+    def twice(n):
+        L = "lk%d" % n
+        for i in range(2):
+            act(A("kk", K24 * i, K24 * (i + 1)), A(L, K24, 2 * K24))
+        act(A("pr", 0, K24), A("pr", K24, 2 * K24))
+        act(A("pr", 3 * K24, 4 * K24), A("pr", 2 * K24, 3 * K24))
+
+    quant(A("uq"), A("us"), A("ut"))
+    src = (T.uq[:, 0:128].bitcast(dt.uint32).indirect(T.ulist16[:, 0:16]), [("uq", 0, 128, 1), ("ulist16", 0, 16, 1)])
+    dst = (T.uq2[:, 0:256].bitcast(dt.uint32), [("uq2", 0, 256, 1)])
+    vcopy(dst, src)
+    psrc = (T.us[:, 0:128].indirect(T.ulist16[:, 0:16]), [("us", 0, 128, 1), ("ulist16", 0, 16, 1)])
+    act(A("us2"), psrc)
+    iota(A("jj"), [[0, K24], [1, 16]], 0, small=True)
+    iota(A("nat"), [[1, C]], 0, small=True)
+    send_children(1)
+    op("g", lambda: g.affine_select(T.eye[:], T.one[:], [[-1, 128]], OP.is_equal, 0.0, 0, 1), [A("eye")], [A("one")])
+
+    def signs(x, h, between=None):
+        lo, hi = HC * h, HC * (h + 1)
+        quant(A("xq", lo, hi), A("xs", lo, hi), A(x, 4 * lo, 4 * hi))
+        mm("ps%d" % (5 - h), "uq2", "us2", 0, "xq", "xs", lo, hi)
+        if h == 0:
+            mm("ps6", "uq2", "us2", 128, "xq", "xs", lo, hi)
+        if between is not None:
+            between()
+        ts(A("b", lo, hi), A("ps%d" % (5 - h), 0, HC), 0.0, OP.is_gt)
+
+    act(A("rst"), A("jj"), AF.Sign)
+    lists_of(0, True)
+    signs("x0", 1)
+
+    def select(m, mp, msum, pr, k, sq, n, out):
+        ts(A(m, 0, n), sq, 2.0, OP.is_lt)
+        ts(A(m, n, 2 * n), sq, 9.0, OP.is_equal)
+        tt(A(mp, 0, 2 * n), A(m, 0, 2 * n), pr, OP.mult)
+        tt(A(msum, 0, n), A(mp, 0, n), A(mp, n, 2 * n), OP.add)
+        tt(out, A(msum, 0, n), k, OP.add)
+
+    for r in range(1, ROUNDS + 1):
+        x, xn = "x%d" % (r - 1), "x%d" % r
+        lu = "lu%d" % (r - 1)
+        fl = (lu, 0, K24)
+        fk = (lu, K24, 2 * K24)
+
+        def pgather(h, t):
+            act(A("pp", 4 * HC * h + t, 4 * HC * (h + 1), 4), IND(x, "la%d" % t, K12 * h, K12 * (h + 1)))
+
+        def padd(h):
+            load("g", A("pp", 4 * HC * h, 4 * HC * (h + 1)), A(x, 4 * HC * h, 4 * HC * (h + 1)), "pa%d_%d" % (r, h), accum_op=OP.add)
+
+        signs(x, 0, lambda: pairs_of(r - 1))
+        pgather(0, 0)
+        pgather(0, 1)
+        act(A("ga", 0, HC), IND("b", lu, 0, K12), AF.Identity, scale=-3.0, bias=3.0)
+        pgather(0, 2)
+        pgather(0, 3)
+        padd(0)
+        ts(A("ga", HC, C), IND("b", lu, K12, K24), -3.0, OP.mult, 3.0, OP.add)
+        tt(A("tx", HC, C), IND("b", lu, K24 + K12, 2 * K24), A("ga", HC, C), OP.add)
+        tt(A("tx", 0, HC), IND("b", lu, K24, K24 + K12), A("ga", 0, HC), OP.add)
+        pgather(1, 0)
+        act(A("c3"), A("tx", 0, C), AF.Relu, scale=-3.0, bias=3.0)
+        ts(A("c0"), A("tx", 0, C), 0.0, OP.is_equal)
+        tt(A("yy"), IND("c0", *fk), A("tx", 0, C), OP.subtract)
+        pgather(1, 1)
+        pgather(1, 2)
+        pgather(1, 3)
+        padd(1)
+        tt(A("tx", C, 768), IND("c3", *fl), A("yy"), OP.add)
+        ts(A("c1"), A("tx", C, 768), 0.0, OP.is_equal)
+        act(A("gb"), IND("c1", *fl), AF.Copy, scale=3.0)
+        if r == 1:
+            for b in range(4):
+                act(A("et", 512 * b + b, 512 * (b + 1), 4), A("eye"))
+        twice(r - 1)
+        act(A("ts"), A("ps6", 0, HC), AF.Sign, scale=-1.0)
+        scan(A("raw"), A("wgt"), A("tx"))
+        ts(A("xi"), A("raw", *VIEW48), A("fac", 0, 1), OP.mult)
+        tt(A("sq"), A("xi"), A("xi"), OP.mult)
+        select("mm", "mp", "ms", A("pr"), A("kk"), A("sq"), 2 * K24, A("d01"))
+        act(A("dn"), IND("nat", "d01", 0, K24))
+        act(A("qn"), IND("dn", "d01", K24, 2 * K24))
+        tt(A("xx"), IND("c1", *fk), A("gb"), OP.add)
+        scan(A("raw2"), A("wgt", 0, C), A("xx"))
+        ts(A("xj"), A("raw2", *VIEW24), A("fac", 0, 1), OP.mult)
+        tt(A("xd"), A("xj"), A("xi", 0, K24), OP.subtract)
+        tt(A("sq2"), A("xd"), A("xd"), OP.mult)
+        select("mm2", "mp2", "ms2", A("pr", K24, 3 * K24), A("kk", 0, K24), A("sq2"), K24, A("d2"))
+        tt(A("om"), IND("qn", "d2", 0, K24), A("sel"), OP.mult)
+        act(A("on"), IND("qn", "d2", 0, K24))
+        scan(A("ow"), A("rst"), A("om"))
+        for t in (2, 3, 0, 1):
+            ts(A("of%d" % t), A("ow", *VIEW24), 4.0, OP.mult, float(t), OP.add)
+        if r == 1:
+            quant(A("eq"), A("es"), A("et"))
+
+        def places():
+            tt(A("mn"), IND("on", "kin%d" % r, 0, K24), A("sel"), OP.mult)
+            scan(A("mw"), A("rst"), A("mn"))
+            vcopy(A("mu"), A("mw", *VIEW24))
+            send(A("min%d" % r), A("mu", K12, K24), partner(r), "rm%d" % r, "lm%d" % r)
+
+        if EARLY:
+            places()
+        for h in (0, 1):
+            for t in (0, 1):
+                ts(A("zt", 4 * HC * h + t, 4 * HC * (h + 1), 4), IND("pp", "of%d" % t, K12 * h, K12 * (h + 1)), 0.5, OP.mult)
+                act(A("zt", 4 * HC * h + t + 2, 4 * HC * (h + 1), 4), IND("pp", "of%d" % (t + 2), K12 * h, K12 * (h + 1)), AF.Copy, scale=0.5)
+            quant(A("zq", HC * h, HC * (h + 1)), A("zs", HC * h, HC * (h + 1)), A("zt", 4 * HC * h, 4 * HC * (h + 1)))
+            for b in range(4):
+                mm("ps%d" % (4 * h + b), "wq", "wp", 128 * b, "zq", "zs", HC * h, HC * (h + 1))
+        if not EARLY:
+            places()
+        for b in range(4):
+            act(A("h%d" % b, 0, HC), A("ps%d" % b, 0, HC), scale=0.03125)
+        for b in (0, 2):
+            ts(A("h%d" % b, HC, C), A("ps%d" % (4 + b), 0, HC), 0.03125, OP.mult)
+            act(A("h%d" % (b + 1), HC, C), A("ps%d" % (5 + b), 0, HC), scale=0.03125)
+            vcopy(A("ht", b, 4 * HC, 4), IND("h%d" % b, "mu", 0, K12))
+            act(A("ht", b + 1, 4 * HC, 4), IND("h%d" % (b + 1), "mu", 0, K12))
+        quant(A("hq"), A("hs"), A("ht"))
+        send((T["dq%d" % r][:, 0:HC].bitcast(dt.uint8), [("dq%d" % r, 0, HC, 1)]), U8("hq", 0, HC), partner(r), "rc%d" % r, "lc%d" % r)
+        send(A("ds%d" % r), A("hs"), partner(r), "rs%d" % r, "ls%d" % r)
+        for b in range(4):
+            tt(A(xn, 4 * HC + b, 8 * HC, 4), IND("h%d" % b, "min%d" % r, 0, K12), A(x, 4 * HC + b, 8 * HC, 4), OP.add)
+        L, Ln = "lk%d" % (r - 1), "lk%d" % r
+        if r < ROUNDS:
+            signs(xn, 1)
+        else:
+            quant(A("xq", HC, C), A("xs", HC, C), A(xn, 4 * HC, 8 * HC))
+        scan(A("tw"), A("wgt", 0, HC), A("ts"))
+        for i in range(2):
+            ts(A("tt", K12 * i, K12 * (i + 1)), A("tw", *VIEW12), A("fac", 0, 1), OP.mult, 0.5, OP.is_gt)
+        tt(A("ud"), A("tt"), A("dif"), OP.mult)
+        tt(A(Ln, 0, K24), A(L, 0, K24), A("ud"), OP.add)
+        tt(A(Ln, 3 * K12, 4 * K12), A(L, 3 * K12, 4 * K12), A("ud", 0, K12), OP.subtract)
+        tt(A(Ln, 2 * K12, 3 * K12), A(L, 2 * K12, 3 * K12), A("ud", K12, K24), OP.subtract)
+        if r < ROUNDS:
+            lists_of(r, False)
+            send_children(r + 1)
+        else:
+            quant(A("vq"), A("vs"), A("vt"))
+            mm("ps4", "vq", "vs", 0, "xq", "xs", HC, C)
+            act(A("yo", HC, C), A("ps4", 0, HC))
+            vcopy(A("lu%d" % r), A(Ln))
+            act(A("lro"), IND("nat", "lu%d" % r, 0, 2 * K24))
+            load("y", X(T.oc[:, 4 * HC:4 * C]), U8("xq", HC, C), "o0")
+            for k in range(4):
+                load("y", X(T.osc[4 * k:4 * k + 4, HC:C]), (T.xs[32 * k:32 * k + 4, HC:C], [("xs", HC, C, 1)]), "o%d" % (1 + k))
+            load("y", X(T.y[:, HC:C]), A("yo", HC, C), "o5")
+            for k in range(8):
+                load("y", X(T.lr[k:k + 1, :]), (T.lro[16 * k:16 * k + 1, :], [("lro", 0, 2 * C, 1)]), "o%d" % (6 + k))
+        for b in range(4):
+            mm("ps%d" % b, "eq", "es", 128 * b, "dq%d" % r, "ds%d" % r, 0, HC)
+            tt(A(xn, b, 4 * HC, 4), A("ps%d" % b, 0, HC), A(x, b, 4 * HC, 4), OP.add)
+
+    quant(A("xq", 0, HC), A("xs", 0, HC), A("x3", 0, 4 * HC))
+    mm("ps5", "vq", "vs", 0, "xq", "xs", 0, HC)
+    load("s", X(T.oc[:, 0:4 * HC]), U8("xq", 0, HC), "o14")
+    for k in range(4):
+        load("y" if k < 2 else "s", X(T.osc[4 * k:4 * k + 4, 0:HC]), (T.xs[32 * k:32 * k + 4, 0:HC], [("xs", 0, HC, 1)]), "o%d" % (15 + k))
+    vcopy(A("yo", 0, HC), A("ps5", 0, HC))
+    load("y", X(T.y[:, 0:HC]), A("yo", 0, HC), "o19")
+    for sem in sorted(total):
+        if known["g"].get(sem, 0) < total[sem]:
+            g.wait_ge(T.sem[sem], total[sem])

@@ -6,143 +6,68 @@ AF = ActivationFunctionType
 C, HC, K24, K12 = 384, 192, 24, 12
 MASK = [1, 2, 3]
 ROUNDS = 3
-EARLY = False
-WGT = 256.0
+WGT = 1024.0
+CYCLE, WAKE, LOOK = 0.00083, 0.12, 0.5
+BOOST = (3.0, 0.0)
 
-SCRATCH = {
-    "x0": ("sbuf", [128, 4 * C], "bfloat16"),
-    "x1": ("sbuf", [128, 4 * C], "bfloat16"),
-    "x2": ("sbuf", [128, 4 * C], "bfloat16"),
-    "x3": ("sbuf", [128, 4 * C], "bfloat16"),
-    "xq": ("sbuf", [128, C], "float8_e4m3fn_x4"),
-    "xs": ("sbuf", [128, C], "uint8"),
-    "pp": ("sbuf", [128, 4 * C], "bfloat16"),
-    "zt": ("sbuf", [128, 4 * C], "bfloat16"),
-    "zq": ("sbuf", [128, C], "float8_e4m3fn_x4"),
-    "zs": ("sbuf", [128, C], "uint8"),
-    "h0": ("sbuf", [128, C], "bfloat16"),
-    "h1": ("sbuf", [128, C], "bfloat16"),
-    "h2": ("sbuf", [128, C], "bfloat16"),
-    "h3": ("sbuf", [128, C], "bfloat16"),
-    "ht": ("sbuf", [128, 4 * HC], "bfloat16"),
-    "hq": ("sbuf", [128, HC], "float8_e4m3fn_x4"),
-    "hs": ("sbuf", [128, HC], "uint8"),
-    "ut": ("sbuf", [128, 512], "bfloat16"),
-    "uq": ("sbuf", [128, 128], "float8_e4m3fn_x4"),
-    "us": ("sbuf", [128, 128], "uint8"),
-    "uq2": ("sbuf", [128, 256], "float8_e4m3fn_x4"),
-    "us2": ("sbuf", [128, 256], "uint8"),
-    "vt": ("sbuf", [128, 512], "bfloat16"),
-    "vq": ("sbuf", [128, 128], "float8_e4m3fn_x4"),
-    "vs": ("sbuf", [128, 128], "uint8"),
-    "wq": ("sbuf", [128, 512], "float8_e4m3fn_x4"),
-    "wp": ("sbuf", [128, 512], "uint8"),
-    "one": ("sbuf", [128, 128], "bfloat16"),
-    "eye": ("sbuf", [128, 128], "bfloat16"),
-    "et": ("sbuf", [128, 2048], "bfloat16"),
-    "eq": ("sbuf", [128, 512], "float8_e4m3fn_x4"),
-    "es": ("sbuf", [128, 512], "uint8"),
-    "ulist": ("sbuf", [128, 16], "int32"),
-    "ulist16": ("sbuf", [128, 16], "uint16"),
-    "ddi": ("sbuf", [128, 16], "int32"),
-    "ddm": ("sbuf", [128, 16], "int32"),
-    "wga": ("sbuf", [128, 16], "bfloat16"),
-    "wgb": ("sbuf", [128, 16], "bfloat16"),
-    "wgt": ("sbuf", [128, 768], "bfloat16"),
-    "sel": ("sbuf", [128, C], "float32"),
-    "jj": ("sbuf", [128, C], "float32"),
-    "rst": ("sbuf", [128, C], "float32"),
-    "nat": ("sbuf", [128, C], "float32"),
-    "pi": ("sbuf", [128, K24], "int32"),
-    "pm": ("sbuf", [128, K24], "int32"),
-    "q16": ("sbuf", [128, K24], "int32"),
-    "cw": ("sbuf", [128, K24], "float32"),
-    "last": ("sbuf", [128, 4], "float32"),
-    "fac": ("sbuf", [128, 4], "float32"),
-    "gin": ("sbuf", [128, 2 * K24], "int32"),
-    "lk0": ("sbuf", [128, 2 * K24], "float32"),
-    "lk1": ("sbuf", [128, 2 * K24], "float32"),
-    "lk2": ("sbuf", [128, 2 * K24], "float32"),
-    "lk3": ("sbuf", [128, 2 * K24], "float32"),
-    "lu0": ("sbuf", [128, 2 * K24], "uint16"),
-    "lu1": ("sbuf", [128, 2 * K24], "uint16"),
-    "lu2": ("sbuf", [128, 2 * K24], "uint16"),
-    "lu3": ("sbuf", [128, 2 * K24], "uint16"),
-    "la0": ("sbuf", [128, K24], "uint16"),
-    "la1": ("sbuf", [128, K24], "uint16"),
-    "la2": ("sbuf", [128, K24], "uint16"),
-    "la3": ("sbuf", [128, K24], "uint16"),
-    "pr": ("sbuf", [128, 4 * K24], "float32"),
-    "kk": ("sbuf", [128, 2 * K24], "float32"),
-    "dif": ("sbuf", [128, K24], "float32"),
-    "tt": ("sbuf", [128, K24], "float32"),
-    "ud": ("sbuf", [128, K24], "float32"),
-    "b": ("sbuf", [128, C], "bfloat16"),
-    "ga": ("sbuf", [128, C], "bfloat16"),
-    "tx": ("sbuf", [128, 768], "bfloat16"),
-    "c0": ("sbuf", [128, C], "bfloat16"),
-    "c3": ("sbuf", [128, C], "bfloat16"),
-    "c1": ("sbuf", [128, C], "bfloat16"),
-    "yy": ("sbuf", [128, C], "bfloat16"),
-    "gb": ("sbuf", [128, C], "bfloat16"),
-    "xx": ("sbuf", [128, C], "bfloat16"),
-    "raw": ("sbuf", [128, 768], "bfloat16"),
-    "raw2": ("sbuf", [128, C], "bfloat16"),
-    "xi": ("sbuf", [128, 2 * K24], "int32"),
-    "sq": ("sbuf", [128, 2 * K24], "float32"),
-    "mm": ("sbuf", [128, 4 * K24], "float32"),
-    "mp": ("sbuf", [128, 4 * K24], "float32"),
-    "ms": ("sbuf", [128, 2 * K24], "float32"),
-    "d01": ("sbuf", [128, 2 * K24], "uint16"),
-    "xj": ("sbuf", [128, K24], "int32"),
-    "xd": ("sbuf", [128, K24], "float32"),
-    "sq2": ("sbuf", [128, K24], "float32"),
-    "mm2": ("sbuf", [128, 2 * K24], "float32"),
-    "mp2": ("sbuf", [128, 2 * K24], "float32"),
-    "ms2": ("sbuf", [128, K24], "float32"),
-    "d2": ("sbuf", [128, K24], "uint16"),
-    "dn": ("sbuf", [128, C], "float32"),
-    "qn": ("sbuf", [128, C], "float32"),
-    "on": ("sbuf", [128, C], "float32"),
-    "om": ("sbuf", [128, C], "float32"),
-    "ow": ("sbuf", [128, C], "float32"),
-    "of0": ("sbuf", [128, K24], "uint16"),
-    "of1": ("sbuf", [128, K24], "uint16"),
-    "of2": ("sbuf", [128, K24], "uint16"),
-    "of3": ("sbuf", [128, K24], "uint16"),
-    "mn": ("sbuf", [128, C], "float32"),
-    "mw": ("sbuf", [128, C], "float32"),
-    "mu": ("sbuf", [128, K24], "uint16"),
-    "ts": ("sbuf", [128, HC], "bfloat16"),
-    "tw": ("sbuf", [128, HC], "bfloat16"),
-    "kin1": ("sbuf", [128, K24], "uint16"),
-    "kin2": ("sbuf", [128, K24], "uint16"),
-    "kin3": ("sbuf", [128, K24], "uint16"),
-    "min1": ("sbuf", [128, K12], "uint16"),
-    "min2": ("sbuf", [128, K12], "uint16"),
-    "min3": ("sbuf", [128, K12], "uint16"),
-    "dq1": ("sbuf", [128, HC], "float8_e4m3fn_x4"),
-    "dq2": ("sbuf", [128, HC], "float8_e4m3fn_x4"),
-    "dq3": ("sbuf", [128, HC], "float8_e4m3fn_x4"),
-    "ds1": ("sbuf", [128, HC], "uint8"),
-    "ds2": ("sbuf", [128, HC], "uint8"),
-    "ds3": ("sbuf", [128, HC], "uint8"),
-    "yo": ("sbuf", [128, C], "float32"),
-    "lro": ("sbuf", [128, 2 * C], "float32"),
-    "ps0": ("psum", [128, 512], "float32"),
-    "ps1": ("psum", [128, 512], "float32"),
-    "ps2": ("psum", [128, 512], "float32"),
-    "ps3": ("psum", [128, 512], "float32"),
-    "ps4": ("psum", [128, 512], "float32"),
-    "ps5": ("psum", [128, 512], "float32"),
-    "ps6": ("psum", [128, 512], "float32"),
-    "ps7": ("psum", [128, 512], "float32"),
-}
+BF, F32, I32, U16, COD, PLN = "bfloat16", "float32", "int32", "uint16", "float8_e4m3fn_x4", "uint8"
+
+
+def _buffers():
+    s = {}
+
+    def sb(dtype, n, *names):
+        for name in names:
+            s[name] = ("sbuf", [128, n], dtype)
+    sb(BF, 4 * C, "x0", "x1", "x2", "x3", "pp", "zt")
+    sb(BF, C, "h0", "h1", "h2", "h3")
+    sb(BF, 4 * HC, "ht")
+    sb(COD, C, "xq", "zq")
+    sb(PLN, C, "xs", "zs")
+    sb(COD, HC, "hq", "dq1", "dq2", "dq3")
+    sb(PLN, HC, "hs", "ds1", "ds2", "ds3")
+    sb(BF, 512, "ut", "vt")
+    sb(COD, 128, "uq", "vq")
+    sb(PLN, 128, "us", "vs")
+    sb(COD, 256, "uq2")
+    sb(PLN, 256, "us2")
+    sb(COD, 512, "wq", "eq")
+    sb(PLN, 512, "wp", "es")
+    sb(BF, 128, "one", "eye")
+    sb(BF, 2048, "et")
+    sb(I32, 16, "ulist", "ddi", "ddm")
+    sb(U16, 16, "ulist16")
+    sb(BF, 16, "wga", "wgb")
+    sb(BF, C, "wgt")
+    sb(F32, C, "sel", "jj", "rst", "nat")
+    sb(I32, K24, "pi", "pm", "q16")
+    sb(F32, K24, "cw")
+    sb(F32, 4, "last", "fac")
+    sb(I32, 2 * K24, "gin")
+    sb(F32, 2 * K24, "lk0", "lk1", "lk2", "lk3")
+    sb(U16, 2 * K24, "lu0", "lu1", "lu2", "lu3")
+    sb(U16, K24, "la0", "la1", "la2", "la3")
+    sb(F32, 3 * K24, "pr")
+    sb(F32, K24, "dif", "tt", "ud", "xd")
+    sb(BF, C, "b", "ga", "c0", "c3", "c1", "yy", "gb", "xx", "raw0", "raw1", "raw2")
+    sb(BF, 2 * C, "tx")
+    sb(F32, 9 * K24, "sm0", "sm1", "sm2")
+    sb(U16, K24, "d0", "d1", "d2", "of0", "of1", "of2", "of3", "mu", "kin1", "kin2", "kin3")
+    sb(U16, K12, "min1", "min2", "min3")
+    sb(F32, C, "dn", "qn", "on", "om", "ow", "mn", "mw", "yo")
+    sb(BF, HC, "ts", "tw")
+    sb(F32, 2 * C, "lro")
+    for i in range(8):
+        s["ps%d" % i] = ("psum", [128, 512], F32)
+    return s
+
+
+SCRATCH = _buffers()
 SEMAPHORES = ["cv", "cs", "ct", "cg"]
-SEMAPHORES += ["i%d" % i for i in range(10)]
+SEMAPHORES += ["i%d" % i for i in range(7)]
 SEMAPHORES += ["pa%d_%d" % (r, h) for r in (1, 2, 3) for h in (0, 1)]
 SEMAPHORES += [n + "%d" % r for r in (1, 2, 3) for n in ("rk", "rm", "rc", "rs", "lk", "lm", "lc", "ls")]
-SEMAPHORES += ["o%d" % i for i in range(24)]
+SEMAPHORES += ["o%d" % i for i in range(20)]
 
 COMPUTE = {"v": "cv", "s": "cs", "t": "ct", "g": "cg"}
 
@@ -152,8 +77,6 @@ def rank_program(g, core, T, topo):
     if rank is None:
         return
     queue = {"v": g.vector, "s": g.scalar, "t": g.tensor, "y": g.sync, "g": g}
-    total = {}
-    known = {q: {} for q in queue}
     seen = {}
 
     def A(name, lo=0, hi=None, step=1):
@@ -170,76 +93,147 @@ def rank_program(g, core, T, topo):
         n = T[win].shape[1]
         return (T[win][:, 0:n].indirect(T[off][:, a:b]), [(win, 0, n, 1), (off, a, b, 1)])
 
+    nodes = []
+    boost = [0.0]
+
     def clash(p, q):
         if p[0] >= q[1] or q[0] >= p[1]:
             return False
         return not (p[2] == 4 and q[2] == 4 and (p[0] - q[0]) % 4)
 
-    def learn(q, sem, val, clock):
-        k = known[q]
-        k[sem] = max(k.get(sem, 0), val)
-        for s, v in clock.items():
-            if v > k.get(s, 0):
-                k[s] = v
-
-    def order(q, reads, writes):
-        need = []
+    def add(q, call, outs, ins, sem, inc, busy, late, slow, after=()):
+        reads = [r for _, regs in ins for r in regs]
+        writes = [r for _, regs in outs for r in regs]
+        me = len(nodes)
+        deps = {n: True for n in after}
         for w, regs in ((False, reads), (True, writes)):
             for name, lo, hi, step in regs:
                 bank = name[:2] == "ps"
-                for (reg, rw, rq, sem, val, clock, slow) in seen.get(name, ()):
-                    if not (w or rw or (bank and rq != q)):
-                        continue
-                    if rq == q and not slow and not rw:
+                for (reg, rw, n) in seen.get(name, ()):
+                    other = nodes[n]
+                    if not (w or rw or (bank and other["q"] != q)):
                         continue
                     if bank or clash(reg, (lo, hi, step)):
-                        if known[q].get(sem, 0) < val:
-                            need.append((val, sem, clock))
-        best = {}
-        for val, sem, clock in need:
-            if sem not in best or best[sem][0] < val:
-                best[sem] = (val, clock)
-        todo = []
-        for sem, (val, clock) in best.items():
-            if not any(s2 != sem and c2.get(sem, 0) >= val for s2, (v2, c2) in best.items()):
-                todo.append((sem, val, clock))
-        for sem, val, clock in todo:
-            queue[q].wait_ge(T.sem[sem], val)
-            learn(q, sem, val, clock)
-
-    def note(q, reads, writes, sem, val, clock, slow):
+                        strong = other["q"] != q or other["slow"] or rw
+                        deps[n] = deps.get(n, False) or strong
         for w, regs in ((False, reads), (True, writes)):
             for name, lo, hi, step in regs:
-                seen.setdefault(name, []).append(((lo, hi, step), w, q, sem, val, clock, slow))
+                seen.setdefault(name, []).append(((lo, hi, step), w, me))
+        nodes.append({"q": q, "call": call, "deps": deps, "sem": sem, "inc": inc, "busy": busy, "late": late, "slow": slow,
+                      "boost": boost[0]})
+        return me
 
-    def op(q, call, outs, ins):
-        reads = [r for _, regs in ins for r in regs]
-        writes = [r for _, regs in outs for r in regs]
-        order(q, reads, writes)
-        sem = COMPUTE[q]
-        total[sem] = total.get(sem, 0) + 1
-        call().then_inc(T.sem[sem], 1)
-        note(q, reads, writes, sem, total[sem], dict(known[q]), False)
+    def width(regs):
+        name, lo, hi, step = regs[0]
+        return (hi - lo + step - 1) // step
+
+    def narrow(regs):
+        return SCRATCH[regs[0][0]][2] == BF
+
+    def op(q, call, outs, ins, pairs=False, flat=False, product=False):
+        n = width(outs[0][1])
+        if product:
+            busy = (n + 16) * CYCLE * 1.4
+        elif flat:
+            busy = 0.012 + 0.00022 * 1.25 * width(ins[0][1])
+        elif any(len(a[1]) > 1 for a in ins):
+            busy = 0.06 + n * CYCLE * 1.6
+        elif q == "s":
+            busy = 0.08 + n * CYCLE * 1.25
+        elif q == "g":
+            busy = 0.15 + 2 * n * CYCLE * 1.25
+        else:
+            both = all(narrow(a[1]) for a in ins + outs)
+            per = 2.0 if pairs and ins[0][1][0][0][:2] != "ps" else 0.5 if both and not pairs else 1.0
+            busy = max(64, n * per) * CYCLE * 1.25
+        add(q, lambda: call().then_inc(T.sem[COMPUTE[q]], 1), outs, ins, COMPUTE[q], 1, busy, 0.0, False)
 
     def load(q, out, in_, sem, **kw):
-        order(q, in_[1], out[1])
-        total[sem] = total.get(sem, 0) + 16
-        queue[q].dma_start(out[0], in_[0], **kw).then_inc(T.sem[sem], 16)
-        note(q, in_[1], out[1], sem, total[sem], dict(known[q]), True)
+        add(q, lambda: queue[q].dma_start(out[0], in_[0], **kw).then_inc(T.sem[sem], 16), [out], [in_], sem, 16,
+            0.6 if q == "g" else 0.06, 2.3, True)
 
     def X(ap):
         return (ap, [])
 
-    def send(out, in_, dst, rsem, lsem):
-        order("g", in_[1], [])
+    def send(out, in_, dst, rsem, lsem, late):
         rid, pid = topo.addr(dst)[:2]
         n = len(topo.engines(core, dst))
-        g.remote_dma(out_ap=out[0], in_ap=in_[0], remote_sem=T.sem[rsem], local_sem=T.sem[lsem],
-                     pid=pid, routing_id=rid, dma_engine_mask=topo.mask(core, dst))
-        total[lsem] = total.get(lsem, 0) + n
-        note("g", in_[1], [], lsem, total[lsem], dict(known["g"]), True)
-        total[rsem] = total.get(rsem, 0) + len(topo.engines(dst, core))
-        note("far", [], out[1], rsem, total[rsem], {}, True)
+        me = add("g", lambda: g.remote_dma(out_ap=out[0], in_ap=in_[0], remote_sem=T.sem[rsem], local_sem=T.sem[lsem],
+                                           pid=pid, routing_id=rid, dma_engine_mask=topo.mask(core, dst)),
+                 [], [in_], lsem, n, 0.6, late, True)
+        add("far", None, [out], [], rsem, len(topo.engines(dst, core)), 0.0, 0.0, True, (me,))
+
+    def plan():
+        after = [[] for _ in nodes]
+        for i, n in enumerate(nodes):
+            for d, strong in n["deps"].items():
+                after[d].append((i, strong))
+        way = [0.0] * len(nodes)
+        for i in range(len(nodes) - 1, -1, -1):
+            own = nodes[i]["busy"] + nodes[i]["late"]
+            way[i] = max([own] + [(own + WAKE if strong else 0.0) + way[j] for j, strong in after[i]])
+        way = [w + n["boost"] for w, n in zip(way, nodes)]
+        left = [len(n["deps"]) for n in nodes]
+        ready = [0.0] * len(nodes)
+        free = {q: 0.0 for q in list(queue) + ["far"]}
+        avail = {q: [] for q in free}
+        for i, n in enumerate(nodes):
+            if not left[i]:
+                avail[n["q"]].append(i)
+        done = []
+        while len(done) < len(nodes):
+            best = None
+            for q, c in avail.items():
+                if not c:
+                    continue
+                now = min(ready[i] for i in c)
+                if q != "far":
+                    now = max(free[q], now)
+                i = max((i for i in c if ready[i] <= now + 1e-9), key=lambda i: (way[i], -i))
+                for j in sorted((j for j in c if ready[j] > now and way[j] > way[i]), key=lambda j: -way[j]):
+                    if ready[j] - now < LOOK * (now + nodes[i]["busy"] - ready[j]):
+                        i, now = j, ready[j]
+                        break
+                if best is None or now < best[0]:
+                    best = (now, q, i)
+            now, q, i = best
+            avail[q].remove(i)
+            free[q] = now + nodes[i]["busy"]
+            done.append(i)
+            end = now + nodes[i]["busy"] + nodes[i]["late"]
+            for j, strong in after[i]:
+                ready[j] = max(ready[j], end + WAKE if strong else now)
+                left[j] -= 1
+                if not left[j]:
+                    avail[nodes[j]["q"]].append(j)
+        return done
+
+    def issue(sequence):
+        known = {q: {} for q in list(queue) + ["far"]}
+        total, value, clock = {}, {}, {}
+        for i in sequence:
+            n = nodes[i]
+            best = {}
+            for d, strong in n["deps"].items():
+                sem = nodes[d]["sem"]
+                if strong and known[n["q"]].get(sem, 0) < value[d] and (sem not in best or value[best[sem]] < value[d]):
+                    best[sem] = d
+            if n["call"] is not None:
+                for sem, d in best.items():
+                    if any(s2 != sem and clock[d2].get(sem, 0) >= value[d] for s2, d2 in best.items()):
+                        continue
+                    queue[n["q"]].wait_ge(T.sem[sem], value[d])
+                    k = known[n["q"]]
+                    for s, v in list(clock[d].items()) + [(sem, value[d])]:
+                        if v > k.get(s, 0):
+                            k[s] = v
+                n["call"]()
+            total[n["sem"]] = total.get(n["sem"], 0) + n["inc"]
+            value[i] = total[n["sem"]]
+            clock[i] = dict(known[n["q"]]) if n["call"] is not None else {}
+        for sem in sorted(total):
+            if known["g"].get(sem, 0) < total[sem]:
+                g.wait_ge(T.sem[sem], total[sem])
 
     def ts(out, a, s1, o1, s2=None, o2=None):
         k1 = s1[0] if isinstance(s1, tuple) else s1
@@ -250,10 +244,13 @@ def rank_program(g, core, T, topo):
             op("v", lambda: g.vector.tensor_scalar(out[0], a[0], k1, s2, o1, o2), [out], ins)
 
     def tt(out, a, b, o):
-        op("v", lambda: g.vector.tensor_tensor(out[0], a[0], b[0], o), [out], [a, b])
+        op("v", lambda: g.vector.tensor_tensor(out[0], a[0], b[0], o), [out], [a, b], pairs=True)
 
     def vcopy(out, a):
         op("v", lambda: g.vector.tensor_copy(out[0], a[0]), [out], [a])
+
+    def fill(out, value):
+        op("v", lambda: g.vector.memset(out[0], value), [out], [])
 
     def act(out, a, func=AF.Copy, scale=1.0, bias=0.0):
         more = {k: v for k, v, d in (("bias", bias, 0.0), ("scale", scale, 1.0)) if v != d}
@@ -263,12 +260,12 @@ def rank_program(g, core, T, topo):
         op("v", lambda: g.vector.tensor_tensor_scan(out[0], d0[0], d1[0], 0.0, OP.mult, OP.add), [out], [d0, d1])
 
     def quant(code, plane, a):
-        op("v", lambda: g.vector.quantize_mx(code[0], plane[0], a[0]), [code, plane], [a])
+        op("v", lambda: g.vector.quantize_mx(code[0], plane[0], a[0]), [code, plane], [a], flat=True)
 
     def mm(bank, lhs, lhs_s, a, rhs, rhs_s, lo, hi):
         out, w, ws_ = A(bank, 0, hi - lo), A(lhs, a, a + 128), A(lhs_s, a, a + 128)
         x, xs_ = A(rhs, lo, hi), A(rhs_s, lo, hi)
-        op("t", lambda: g.tensor.matmul_mx(out[0], w[0], ws_[0], x[0], xs_[0], True, True), [out], [w, ws_, x, xs_])
+        op("t", lambda: g.tensor.matmul_mx(out[0], w[0], ws_[0], x[0], xs_[0], True, True), [out], [w, ws_, x, xs_], product=True)
 
     def iota(out, pattern, cm, base=0, small=False):
         if small:
@@ -276,7 +273,7 @@ def rank_program(g, core, T, topo):
         else:
             op("g", lambda: g.iota(out[0], pattern, base, cm), [out], [])
 
-    VIEW48, VIEW24, VIEW12 = (15, 768, 16), (15, C, 16), (15, HC, 16)
+    VIEW24, VIEW12 = (15, C, 16), (15, HC, 16)
 
     load("y", A("ut"), X(T.u[:]), "i0")
     load("s", A("gin", K24, 2 * K24), X(T.gk[:]), "i1")
@@ -292,20 +289,21 @@ def rank_program(g, core, T, topo):
 
     vcopy(A("ulist16"), A("ulist"))
     ts(A("ddm"), A("ddi"), 15, OP.bitwise_and)
-    ts(A("wga"), A("ddm"), 1, OP.is_equal, WGT - 1.0, OP.mult)
-    ts(A("wgb"), A("ddm"), 0, OP.not_equal)
+    ts(A("wga"), A("ddm"), 1, OP.is_equal, WGT, OP.mult)
+    ts(A("wgb"), A("ddm"), 1, OP.is_gt)
     tt(A("wgt", 0, 16), A("wga"), A("wgb"), OP.add)
     ts(A("sel", 0, 16), A("ddm"), 0, OP.is_equal)
     ts(A("pm"), A("pi"), 15, OP.bitwise_and)
     tt(A("cw"), A("pm"), A("q16"), OP.add)
     ts(A("last", 0, 1), A("pm", 0, 1), 15, OP.is_equal)
     ts(A("fac", 0, 1), A("last", 0, 1), 1.0 - 1.0 / WGT, OP.mult, 1.0 / WGT, OP.add)
-    op("v", lambda: g.vector.memset(T.one[:], 1.0), [A("one")], [])
-    op("v", lambda: g.vector.memset(T.et[:], 0.0), [A("et")], [])
-    for name, width in (("wgt", 768), ("sel", C)):
+    ts(A("fac", 1, 2), A("last", 0, 1), 1.0 - WGT ** -2, OP.mult, WGT ** -2, OP.add)
+    fill(A("one"), 1.0)
+    fill(A("et"), 0.0)
+    for name in ("wgt", "sel"):
         have = 16
-        while have < width:
-            more = min(have, width - have)
+        while have < C:
+            more = min(have, C - have)
             act(A(name, have, have + more), A(name, 0, more))
             have += more
     vcopy(A("lu0", K24, 2 * K24), A("gin", K24, 2 * K24))
@@ -314,7 +312,7 @@ def rank_program(g, core, T, topo):
         return T.cores[rank ^ MASK[r - 1]]
 
     def send_children(r):
-        send(A("kin%d" % r), A("lu%d" % (r - 1), K24, 2 * K24), partner(r), "rk%d" % r, "lk%d" % r)
+        send(A("kin%d" % r), A("lu%d" % (r - 1), K24, 2 * K24), partner(r), "rk%d" % r, "lk%d" % r, 2.0)
 
     def lists_of(n, first):
         L = "lk%d" % n
@@ -328,125 +326,102 @@ def rank_program(g, core, T, topo):
 
     def pairs_of(n):
         L = "lk%d" % n
-        tt(A("pr", K24, 2 * K24), A(L, 0, K24), A(L, K24, 2 * K24), OP.subtract)
-        tt(A("pr", 2 * K24, 3 * K24), A("cw"), A(L, K24, 2 * K24), OP.subtract)
+        tt(A("pr", 0, K24), A(L, K24, 2 * K24), A(L, 0, K24), OP.subtract)
+        tt(A("pr", K24, 2 * K24), A("cw"), A(L, K24, 2 * K24), OP.subtract)
+        tt(A("pr", 2 * K24, 3 * K24), A(L, K24, 2 * K24), A("cw"), OP.subtract)
         tt(A("dif", 0, K12), A(L, 3 * K12, 4 * K12), A(L, 0, K12), OP.subtract)
         tt(A("dif", K12, K24), A(L, 2 * K12, 3 * K12), A(L, K12, 2 * K12), OP.subtract)
 
-    def twice(n):
-        L = "lk%d" % n
-        for i in range(2):
-            act(A("kk", K24 * i, K24 * (i + 1)), A(L, K24, 2 * K24))
-        act(A("pr", 0, K24), A("pr", K24, 2 * K24))
-        act(A("pr", 3 * K24, 4 * K24), A("pr", 2 * K24, 3 * K24))
-
     quant(A("uq"), A("us"), A("ut"))
     src = (T.uq[:, 0:128].bitcast(dt.uint32).indirect(T.ulist16[:, 0:16]), [("uq", 0, 128, 1), ("ulist16", 0, 16, 1)])
-    dst = (T.uq2[:, 0:256].bitcast(dt.uint32), [("uq2", 0, 256, 1)])
-    vcopy(dst, src)
-    psrc = (T.us[:, 0:128].indirect(T.ulist16[:, 0:16]), [("us", 0, 128, 1), ("ulist16", 0, 16, 1)])
-    act(A("us2"), psrc)
+    vcopy((T.uq2[:, 0:256].bitcast(dt.uint32), [("uq2", 0, 256, 1)]), src)
+    act(A("us2"), (T.us[:, 0:128].indirect(T.ulist16[:, 0:16]), [("us", 0, 128, 1), ("ulist16", 0, 16, 1)]))
     iota(A("jj"), [[0, K24], [1, 16]], 0, small=True)
     iota(A("nat"), [[1, C]], 0, small=True)
     send_children(1)
     op("g", lambda: g.affine_select(T.eye[:], T.one[:], [[-1, 128]], OP.is_equal, 0.0, 0, 1), [A("eye")], [A("one")])
 
-    def signs(x, h, between=None):
+    def signs(x, h):
         lo, hi = HC * h, HC * (h + 1)
         quant(A("xq", lo, hi), A("xs", lo, hi), A(x, 4 * lo, 4 * hi))
         mm("ps%d" % (5 - h), "uq2", "us2", 0, "xq", "xs", lo, hi)
         if h == 0:
             mm("ps6", "uq2", "us2", 128, "xq", "xs", lo, hi)
-        if between is not None:
-            between()
         ts(A("b", lo, hi), A("ps%d" % (5 - h), 0, HC), 0.0, OP.is_gt)
 
     act(A("rst"), A("jj"), AF.Sign)
     lists_of(0, True)
     signs("x0", 1)
 
-    def select(m, mp, msum, pr, k, sq, n, out):
-        ts(A(m, 0, n), sq, 2.0, OP.is_lt)
-        ts(A(m, n, 2 * n), sq, 9.0, OP.is_equal)
-        tt(A(mp, 0, 2 * n), A(m, 0, 2 * n), pr, OP.mult)
-        tt(A(msum, 0, n), A(mp, 0, n), A(mp, n, 2 * n), OP.add)
-        tt(out, A(msum, 0, n), k, OP.add)
+    def select(s, raw, L):
+        def B(i, n=1):
+            return A("sm" + s, K24 * i, K24 * (i + n))
+        tt(B(0), raw, raw, OP.mult)
+        for i, least in enumerate((2.3, 6.2, 12.2)):
+            ts(B(1 + i), B(0), A("fac", 1, 2), OP.mult, least, OP.is_gt)
+        tt(B(4, 3), B(1, 3), A("pr"), OP.mult)
+        tt(B(7), B(4), B(5), OP.add)
+        tt(B(8), B(6), A(L, 0, K24), OP.add)
+        tt(A("d" + s), B(7), B(8), OP.add)
 
     for r in range(1, ROUNDS + 1):
         x, xn = "x%d" % (r - 1), "x%d" % r
-        lu = "lu%d" % (r - 1)
+        lu, L, Ln = "lu%d" % (r - 1), "lk%d" % (r - 1), "lk%d" % r
         fl = (lu, 0, K24)
         fk = (lu, K24, 2 * K24)
 
-        def pgather(h, t):
-            act(A("pp", 4 * HC * h + t, 4 * HC * (h + 1), 4), IND(x, "la%d" % t, K12 * h, K12 * (h + 1)))
-
-        def padd(h):
+        signs(x, 0)
+        pairs_of(r - 1)
+        for h in (0, 1):
+            for t in range(4):
+                act(A("pp", 4 * HC * h + t, 4 * HC * (h + 1), 4), IND(x, "la%d" % t, K12 * h, K12 * (h + 1)))
             load("g", A("pp", 4 * HC * h, 4 * HC * (h + 1)), A(x, 4 * HC * h, 4 * HC * (h + 1)), "pa%d_%d" % (r, h), accum_op=OP.add)
-
-        signs(x, 0, lambda: pairs_of(r - 1))
-        pgather(0, 0)
-        pgather(0, 1)
         act(A("ga", 0, HC), IND("b", lu, 0, K12), AF.Identity, scale=-3.0, bias=3.0)
-        pgather(0, 2)
-        pgather(0, 3)
-        padd(0)
         ts(A("ga", HC, C), IND("b", lu, K12, K24), -3.0, OP.mult, 3.0, OP.add)
         tt(A("tx", HC, C), IND("b", lu, K24 + K12, 2 * K24), A("ga", HC, C), OP.add)
         tt(A("tx", 0, HC), IND("b", lu, K24, K24 + K12), A("ga", 0, HC), OP.add)
-        pgather(1, 0)
         act(A("c3"), A("tx", 0, C), AF.Relu, scale=-3.0, bias=3.0)
         ts(A("c0"), A("tx", 0, C), 0.0, OP.is_equal)
         tt(A("yy"), IND("c0", *fk), A("tx", 0, C), OP.subtract)
-        pgather(1, 1)
-        pgather(1, 2)
-        pgather(1, 3)
-        padd(1)
-        tt(A("tx", C, 768), IND("c3", *fl), A("yy"), OP.add)
-        ts(A("c1"), A("tx", C, 768), 0.0, OP.is_equal)
+        tt(A("tx", C, 2 * C), IND("c3", *fl), A("yy"), OP.add)
+        ts(A("c1"), A("tx", C, 2 * C), 0.0, OP.is_equal)
         act(A("gb"), IND("c1", *fl), AF.Copy, scale=3.0)
+        tt(A("xx"), IND("c1", *fk), A("gb"), OP.add)
         if r == 1:
             for b in range(4):
                 act(A("et", 512 * b + b, 512 * (b + 1), 4), A("eye"))
-        twice(r - 1)
+            quant(A("eq"), A("es"), A("et"))
         act(A("ts"), A("ps6", 0, HC), AF.Sign, scale=-1.0)
-        scan(A("raw"), A("wgt"), A("tx"))
-        ts(A("xi"), A("raw", *VIEW48), A("fac", 0, 1), OP.mult)
-        tt(A("sq"), A("xi"), A("xi"), OP.mult)
-        select("mm", "mp", "ms", A("pr"), A("kk"), A("sq"), 2 * K24, A("d01"))
-        act(A("dn"), IND("nat", "d01", 0, K24))
-        act(A("qn"), IND("dn", "d01", K24, 2 * K24))
-        tt(A("xx"), IND("c1", *fk), A("gb"), OP.add)
-        scan(A("raw2"), A("wgt", 0, C), A("xx"))
-        ts(A("xj"), A("raw2", *VIEW24), A("fac", 0, 1), OP.mult)
-        tt(A("xd"), A("xj"), A("xi", 0, K24), OP.subtract)
-        tt(A("sq2"), A("xd"), A("xd"), OP.mult)
-        select("mm2", "mp2", "ms2", A("pr", K24, 3 * K24), A("kk", 0, K24), A("sq2"), K24, A("d2"))
+        scan(A("raw0"), A("wgt"), A("tx", 0, C))
+        select("0", A("raw0", *VIEW24), L)
+        act(A("dn"), IND("nat", "d0", 0, K24))
+        scan(A("raw1"), A("wgt"), A("tx", C, 2 * C))
+        select("1", A("raw1", *VIEW24), L)
+        act(A("qn"), IND("dn", "d1", 0, K24))
+        scan(A("raw2"), A("wgt"), A("xx"))
+        tt(A("xd"), A("raw2", *VIEW24), A("raw0", *VIEW24), OP.subtract)
+        select("2", A("xd"), L)
         tt(A("om"), IND("qn", "d2", 0, K24), A("sel"), OP.mult)
         act(A("on"), IND("qn", "d2", 0, K24))
         scan(A("ow"), A("rst"), A("om"))
         for t in (2, 3, 0, 1):
             ts(A("of%d" % t), A("ow", *VIEW24), 4.0, OP.mult, float(t), OP.add)
-        if r == 1:
-            quant(A("eq"), A("es"), A("et"))
-
-        def places():
-            tt(A("mn"), IND("on", "kin%d" % r, 0, K24), A("sel"), OP.mult)
-            scan(A("mw"), A("rst"), A("mn"))
-            vcopy(A("mu"), A("mw", *VIEW24))
-            send(A("min%d" % r), A("mu", K12, K24), partner(r), "rm%d" % r, "lm%d" % r)
-
-        if EARLY:
-            places()
         for h in (0, 1):
-            for t in (0, 1):
-                ts(A("zt", 4 * HC * h + t, 4 * HC * (h + 1), 4), IND("pp", "of%d" % t, K12 * h, K12 * (h + 1)), 0.5, OP.mult)
-                act(A("zt", 4 * HC * h + t + 2, 4 * HC * (h + 1), 4), IND("pp", "of%d" % (t + 2), K12 * h, K12 * (h + 1)), AF.Copy, scale=0.5)
+            boost[0] = BOOST[h]
+            for t in range(4):
+                z, p = A("zt", 4 * HC * h + t, 4 * HC * (h + 1), 4), IND("pp", "of%d" % t, K12 * h, K12 * (h + 1))
+                if t < 2 - h:
+                    ts(z, p, 0.5, OP.mult)
+                else:
+                    act(z, p, AF.Copy, scale=0.5)
             quant(A("zq", HC * h, HC * (h + 1)), A("zs", HC * h, HC * (h + 1)), A("zt", 4 * HC * h, 4 * HC * (h + 1)))
             for b in range(4):
                 mm("ps%d" % (4 * h + b), "wq", "wp", 128 * b, "zq", "zs", HC * h, HC * (h + 1))
-        if not EARLY:
-            places()
+        boost[0] = 0.0
+        tt(A("mn"), IND("on", "kin%d" % r, 0, K24), A("sel"), OP.mult)
+        scan(A("mw"), A("rst"), A("mn"))
+        vcopy(A("mu"), A("mw", *VIEW24))
+        send(A("min%d" % r), A("mu", K12, K24), partner(r), "rm%d" % r, "lm%d" % r, 2.0)
         for b in range(4):
             act(A("h%d" % b, 0, HC), A("ps%d" % b, 0, HC), scale=0.03125)
         for b in (0, 2):
@@ -455,11 +430,10 @@ def rank_program(g, core, T, topo):
             vcopy(A("ht", b, 4 * HC, 4), IND("h%d" % b, "mu", 0, K12))
             act(A("ht", b + 1, 4 * HC, 4), IND("h%d" % (b + 1), "mu", 0, K12))
         quant(A("hq"), A("hs"), A("ht"))
-        send((T["dq%d" % r][:, 0:HC].bitcast(dt.uint8), [("dq%d" % r, 0, HC, 1)]), U8("hq", 0, HC), partner(r), "rc%d" % r, "lc%d" % r)
-        send(A("ds%d" % r), A("hs"), partner(r), "rs%d" % r, "ls%d" % r)
+        send(U8("dq%d" % r, 0, HC), U8("hq", 0, HC), partner(r), "rc%d" % r, "lc%d" % r, 3.0)
+        send(A("ds%d" % r), A("hs"), partner(r), "rs%d" % r, "ls%d" % r, 2.7)
         for b in range(4):
             tt(A(xn, 4 * HC + b, 8 * HC, 4), IND("h%d" % b, "min%d" % r, 0, K12), A(x, 4 * HC + b, 8 * HC, 4), OP.add)
-        L, Ln = "lk%d" % (r - 1), "lk%d" % r
         if r < ROUNDS:
             signs(xn, 1)
         else:
@@ -497,6 +471,4 @@ def rank_program(g, core, T, topo):
         load("y" if k < 2 else "s", X(T.osc[4 * k:4 * k + 4, 0:HC]), (T.xs[32 * k:32 * k + 4, 0:HC], [("xs", 0, HC, 1)]), "o%d" % (15 + k))
     vcopy(A("yo", 0, HC), A("ps5", 0, HC))
     load("y", X(T.y[:, 0:HC]), A("yo", 0, HC), "o19")
-    for sem in sorted(total):
-        if known["g"].get(sem, 0) < total[sem]:
-            g.wait_ge(T.sem[sem], total[sem])
+    issue(plan())

from concourse.bass import DstId, RemoteDMATransfer
from concourse.mybir import dt, AluOpType, ActivationFunctionType

OP = AluOpType
AF = ActivationFunctionType
C, HC, K24, K12 = 384, 192, 24, 12
MASK = [1, 2, 3]
ROUNDS = 3
WGT = 1024.0
CYCLE, WAKE, LOOK = 0.00083, 0.12, 0.5
BOOST = (3.0, 0.0)

BF, F32, I32, U16, COD, PLN = "bfloat16", "float32", "int32", "uint16", "float8_e4m3fn_x4", "uint8"


def _buffers():
    s = {}

    def sb(dtype, n, *names):
        for name in names:
            s[name] = ("sbuf", [128, n], dtype)
    sb(BF, 4 * C, "x0", "x1", "x2", "x3", "pp", "zt")
    sb(BF, C, "h0", "h1", "h2", "h3")
    sb(BF, 4 * HC, "ht")
    sb(COD, C, "xq", "zq")
    sb(PLN, C, "xs", "zs")
    sb(COD, HC, "hq", "dq1", "dq2", "dq3")
    sb(PLN, HC, "hs", "ds1", "ds2", "ds3")
    sb(BF, 512, "ut", "vt")
    sb(COD, 128, "uq", "vq")
    sb(PLN, 128, "us", "vs")
    sb(COD, 256, "uq2")
    sb(PLN, 256, "us2")
    sb(COD, 512, "wq", "eq")
    sb(PLN, 512, "wp", "es")
    sb(BF, 128, "one", "eye")
    sb(BF, 2048, "et")
    sb(I32, 16, "ulist", "ddi", "ddm")
    sb(U16, 16, "ulist16")
    sb(BF, 16, "wga", "wgb")
    sb(BF, C, "wgt")
    sb(F32, C, "sel", "jj", "rst", "nat")
    sb(I32, K24, "pi", "pm", "q16")
    sb(F32, K24, "cw")
    sb(F32, 4, "last", "fac")
    sb(I32, 2 * K24, "gin")
    sb(F32, 2 * K24, "lk0", "lk1", "lk2", "lk3")
    sb(U16, 2 * K24, "lu0", "lu1", "lu2", "lu3")
    sb(U16, K24, "la0", "la1", "la2", "la3")
    sb(F32, 3 * K24, "pr")
    sb(F32, K24, "dif", "tt", "ud", "xd")
    sb(BF, C, "b", "ga", "c0", "c3", "c1", "yy", "gb", "xx", "raw0", "raw1", "raw2")
    sb(BF, 2 * C, "tx")
    sb(F32, 9 * K24, "sm0", "sm1", "sm2")
    sb(U16, K24, "d0", "d1", "d2", "of0", "of1", "of2", "of3", "mu", "kin1", "kin2", "kin3")
    sb(U16, K12, "min1", "min2", "min3")
    sb(F32, C, "dn", "qn", "on", "om", "ow", "mn", "mw", "yo")
    sb(BF, HC, "ts", "tw")
    sb(F32, 2 * C, "lro")
    for i in range(8):
        s["ps%d" % i] = ("psum", [128, 512], F32)
    return s


SCRATCH = _buffers()
SEMAPHORES = ["cv", "cs", "ct", "cg"]
SEMAPHORES += ["i%d" % i for i in range(7)]
SEMAPHORES += ["pa%d_%d" % (r, h) for r in (1, 2, 3) for h in (0, 1)]
SEMAPHORES += [n + "%d" % r for r in (1, 2, 3) for n in ("rk", "rm", "rc", "rs", "lk", "lm", "lc", "ls")]
SEMAPHORES += ["o%d" % i for i in range(20)]

COMPUTE = {"v": "cv", "s": "cs", "t": "ct", "g": "cg"}


def rank_program(g, core, T, topo):
    rank = T.rank_of(core)
    if rank is None:
        return
    queue = {"v": g.vector, "s": g.scalar, "t": g.tensor, "y": g.sync, "g": g}
    seen = {}

    def A(name, lo=0, hi=None, step=1):
        t = T[name]
        n = t.shape[1]
        hi = n if hi is None else hi
        ap = t[:, lo:hi] if step == 1 else t[:, lo:hi:step]
        return (ap, [(name, lo, hi, step)])

    def U8(name, lo, hi):
        return (T[name][:, lo:hi].bitcast(dt.uint8), [(name, lo, hi, 1)])

    def IND(win, off, a, b):
        n = T[win].shape[1]
        return (T[win][:, 0:n].indirect(T[off][:, a:b]), [(win, 0, n, 1), (off, a, b, 1)])

    nodes = []
    boost = [0.0]

    def clash(p, q):
        if p[0] >= q[1] or q[0] >= p[1]:
            return False
        return not (p[2] == 4 and q[2] == 4 and (p[0] - q[0]) % 4)

    def add(q, call, outs, ins, sem, inc, busy, late, slow, after=()):
        reads = [r for _, regs in ins for r in regs]
        writes = [r for _, regs in outs for r in regs]
        me = len(nodes)
        deps = {n: True for n in after}
        for w, regs in ((False, reads), (True, writes)):
            for name, lo, hi, step in regs:
                bank = name[:2] == "ps"
                for (reg, rw, n) in seen.get(name, ()):
                    other = nodes[n]
                    if not (w or rw or (bank and other["q"] != q)):
                        continue
                    if bank or clash(reg, (lo, hi, step)):
                        strong = other["q"] != q or other["slow"] or rw
                        deps[n] = deps.get(n, False) or strong
        for w, regs in ((False, reads), (True, writes)):
            for name, lo, hi, step in regs:
                seen.setdefault(name, []).append(((lo, hi, step), w, me))
        nodes.append({"q": q, "call": call, "deps": deps, "sem": sem, "inc": inc, "busy": busy, "late": late, "slow": slow,
                      "boost": boost[0]})
        return me

    def width(regs):
        name, lo, hi, step = regs[0]
        return (hi - lo + step - 1) // step

    def narrow(regs):
        return SCRATCH[regs[0][0]][2] == BF

    def op(q, call, outs, ins, pairs=False, flat=False, product=False):
        n = width(outs[0][1])
        if product:
            busy = (n + 16) * CYCLE * 1.4
        elif flat:
            busy = 0.012 + 0.00022 * 1.25 * width(ins[0][1])
        elif any(len(a[1]) > 1 for a in ins):
            busy = 0.06 + n * CYCLE * 1.6
        elif q == "s":
            busy = 0.08 + n * CYCLE * 1.25
        elif q == "g":
            busy = 0.15 + 2 * n * CYCLE * 1.25
        else:
            both = all(narrow(a[1]) for a in ins + outs)
            per = 2.0 if pairs and ins[0][1][0][0][:2] != "ps" else 0.5 if both and not pairs else 1.0
            busy = max(64, n * per) * CYCLE * 1.25
        add(q, lambda: call().then_inc(T.sem[COMPUTE[q]], 1), outs, ins, COMPUTE[q], 1, busy, 0.0, False)

    def load(q, out, in_, sem, **kw):
        add(q, lambda: queue[q].dma_start(out[0], in_[0], **kw).then_inc(T.sem[sem], 16), [out], [in_], sem, 16,
            0.6 if q == "g" else 0.06, 2.3, True)

    def X(ap):
        return (ap, [])

    def send(out, in_, dst, rsem, lsem, late):
        rid, pid = topo.addr(dst)[:2]
        n = len(topo.engines(core, dst))
        me = add("g", lambda: g.remote_dma(out_ap=out[0], in_ap=in_[0], remote_sem=T.sem[rsem], local_sem=T.sem[lsem],
                                           pid=pid, routing_id=rid, dma_engine_mask=topo.mask(core, dst)),
                 [], [in_], lsem, n, 0.6, late, True)
        add("far", None, [out], [], rsem, len(topo.engines(dst, core)), 0.0, 0.0, True, (me,))

    def plan():
        after = [[] for _ in nodes]
        for i, n in enumerate(nodes):
            for d, strong in n["deps"].items():
                after[d].append((i, strong))
        way = [0.0] * len(nodes)
        for i in range(len(nodes) - 1, -1, -1):
            own = nodes[i]["busy"] + nodes[i]["late"]
            way[i] = max([own] + [(own + WAKE if strong else 0.0) + way[j] for j, strong in after[i]])
        way = [w + n["boost"] for w, n in zip(way, nodes)]
        left = [len(n["deps"]) for n in nodes]
        ready = [0.0] * len(nodes)
        free = {q: 0.0 for q in list(queue) + ["far"]}
        avail = {q: [] for q in free}
        for i, n in enumerate(nodes):
            if not left[i]:
                avail[n["q"]].append(i)
        done = []
        while len(done) < len(nodes):
            best = None
            for q, c in avail.items():
                if not c:
                    continue
                now = min(ready[i] for i in c)
                if q != "far":
                    now = max(free[q], now)
                i = max((i for i in c if ready[i] <= now + 1e-9), key=lambda i: (way[i], -i))
                for j in sorted((j for j in c if ready[j] > now and way[j] > way[i]), key=lambda j: -way[j]):
                    if ready[j] - now < LOOK * (now + nodes[i]["busy"] - ready[j]):
                        i, now = j, ready[j]
                        break
                if best is None or now < best[0]:
                    best = (now, q, i)
            now, q, i = best
            avail[q].remove(i)
            free[q] = now + nodes[i]["busy"]
            done.append(i)
            end = now + nodes[i]["busy"] + nodes[i]["late"]
            for j, strong in after[i]:
                ready[j] = max(ready[j], end + WAKE if strong else now)
                left[j] -= 1
                if not left[j]:
                    avail[nodes[j]["q"]].append(j)
        return done

    def issue(sequence):
        known = {q: {} for q in list(queue) + ["far"]}
        total, value, clock = {}, {}, {}
        for i in sequence:
            n = nodes[i]
            best = {}
            for d, strong in n["deps"].items():
                sem = nodes[d]["sem"]
                if strong and known[n["q"]].get(sem, 0) < value[d] and (sem not in best or value[best[sem]] < value[d]):
                    best[sem] = d
            if n["call"] is not None:
                for sem, d in best.items():
                    if any(s2 != sem and clock[d2].get(sem, 0) >= value[d] for s2, d2 in best.items()):
                        continue
                    queue[n["q"]].wait_ge(T.sem[sem], value[d])
                    k = known[n["q"]]
                    for s, v in list(clock[d].items()) + [(sem, value[d])]:
                        if v > k.get(s, 0):
                            k[s] = v
                n["call"]()
            total[n["sem"]] = total.get(n["sem"], 0) + n["inc"]
            value[i] = total[n["sem"]]
            clock[i] = dict(known[n["q"]]) if n["call"] is not None else {}
        for sem in sorted(total):
            if known["g"].get(sem, 0) < total[sem]:
                g.wait_ge(T.sem[sem], total[sem])

    def ts(out, a, s1, o1, s2=None, o2=None):
        k1 = s1[0] if isinstance(s1, tuple) else s1
        ins = [a] + ([s1] if isinstance(s1, tuple) else [])
        if o2 is None:
            op("v", lambda: g.vector.tensor_scalar(out[0], a[0], k1, None, o1), [out], ins)
        else:
            op("v", lambda: g.vector.tensor_scalar(out[0], a[0], k1, s2, o1, o2), [out], ins)

    def tt(out, a, b, o):
        op("v", lambda: g.vector.tensor_tensor(out[0], a[0], b[0], o), [out], [a, b], pairs=True)

    def vcopy(out, a):
        op("v", lambda: g.vector.tensor_copy(out[0], a[0]), [out], [a])

    def fill(out, value):
        op("v", lambda: g.vector.memset(out[0], value), [out], [])

    def act(out, a, func=AF.Copy, scale=1.0, bias=0.0):
        more = {k: v for k, v, d in (("bias", bias, 0.0), ("scale", scale, 1.0)) if v != d}
        op("s", lambda: g.scalar.activation(out[0], a[0], func, **more), [out], [a])

    def scan(out, d0, d1):
        op("v", lambda: g.vector.tensor_tensor_scan(out[0], d0[0], d1[0], 0.0, OP.mult, OP.add), [out], [d0, d1])

    def quant(code, plane, a):
        op("v", lambda: g.vector.quantize_mx(code[0], plane[0], a[0]), [code, plane], [a], flat=True)

    def mm(bank, lhs, lhs_s, a, rhs, rhs_s, lo, hi):
        out, w, ws_ = A(bank, 0, hi - lo), A(lhs, a, a + 128), A(lhs_s, a, a + 128)
        x, xs_ = A(rhs, lo, hi), A(rhs_s, lo, hi)
        op("t", lambda: g.tensor.matmul_mx(out[0], w[0], ws_[0], x[0], xs_[0], True, True), [out], [w, ws_, x, xs_], product=True)

    def iota(out, pattern, cm, base=0, small=False):
        if small:
            op("g", lambda: g.iota(out[0], pattern, base, cm, allow_small_or_imprecise_dtypes=True), [out], [])
        else:
            op("g", lambda: g.iota(out[0], pattern, base, cm), [out], [])

    VIEW24, VIEW12 = (15, C, 16), (15, HC, 16)

    load("y", A("ut"), X(T.u[:]), "i0")
    load("s", A("gin", K24, 2 * K24), X(T.gk[:]), "i1")
    load("y", A("x0"), X(T.x[:]), "i2")
    iota(A("ulist"), [[1, 2], [16, 8]], 0)
    iota(A("ddi"), [[1, 16]], -1, base=128)
    iota(A("pi"), [[0, K24]], 1)
    iota(A("q16"), [[16, K24]], 0)
    load("g", A("gin", 0, K24), X(T.gl[:]), "i3")
    load("y", U8("wq", 0, 512), X(T.wc[:]), "i4")
    load("y", A("wp"), X(T.ws[:]), "i5")
    load("y", A("vt"), X(T.v[:]), "i6")

    vcopy(A("ulist16"), A("ulist"))
    ts(A("ddm"), A("ddi"), 15, OP.bitwise_and)
    ts(A("wga"), A("ddm"), 1, OP.is_equal, WGT, OP.mult)
    ts(A("wgb"), A("ddm"), 1, OP.is_gt)
    tt(A("wgt", 0, 16), A("wga"), A("wgb"), OP.add)
    ts(A("sel", 0, 16), A("ddm"), 0, OP.is_equal)
    ts(A("pm"), A("pi"), 15, OP.bitwise_and)
    tt(A("cw"), A("pm"), A("q16"), OP.add)
    ts(A("last", 0, 1), A("pm", 0, 1), 15, OP.is_equal)
    ts(A("fac", 0, 1), A("last", 0, 1), 1.0 - 1.0 / WGT, OP.mult, 1.0 / WGT, OP.add)
    ts(A("fac", 1, 2), A("last", 0, 1), 1.0 - WGT ** -2, OP.mult, WGT ** -2, OP.add)
    fill(A("one"), 1.0)
    fill(A("et"), 0.0)
    for name in ("wgt", "sel"):
        have = 16
        while have < C:
            more = min(have, C - have)
            act(A(name, have, have + more), A(name, 0, more))
            have += more
    vcopy(A("lu0", K24, 2 * K24), A("gin", K24, 2 * K24))

    def partner(r):
        return T.cores[rank ^ MASK[r - 1]]

    def send_children(r):
        send(A("kin%d" % r), A("lu%d" % (r - 1), K24, 2 * K24), partner(r), "rk%d" % r, "lk%d" % r, 2.0)

    def lists_of(n, first):
        L = "lk%d" % n
        if first:
            vcopy(A("lu%d" % n, 0, K24), A("gin", 0, K24))
            vcopy(A(L), A("gin"))
        else:
            vcopy(A("lu%d" % n), A(L))
        for t in range(4):
            ts(A("la%d" % t), A(L, 0, K24), 4.0, OP.mult, float(t), OP.add)

    def pairs_of(n):
        L = "lk%d" % n
        tt(A("pr", 0, K24), A(L, K24, 2 * K24), A(L, 0, K24), OP.subtract)
        tt(A("pr", K24, 2 * K24), A("cw"), A(L, K24, 2 * K24), OP.subtract)
        tt(A("pr", 2 * K24, 3 * K24), A(L, K24, 2 * K24), A("cw"), OP.subtract)
        tt(A("dif", 0, K12), A(L, 3 * K12, 4 * K12), A(L, 0, K12), OP.subtract)
        tt(A("dif", K12, K24), A(L, 2 * K12, 3 * K12), A(L, K12, 2 * K12), OP.subtract)

    quant(A("uq"), A("us"), A("ut"))
    src = (T.uq[:, 0:128].bitcast(dt.uint32).indirect(T.ulist16[:, 0:16]), [("uq", 0, 128, 1), ("ulist16", 0, 16, 1)])
    vcopy((T.uq2[:, 0:256].bitcast(dt.uint32), [("uq2", 0, 256, 1)]), src)
    act(A("us2"), (T.us[:, 0:128].indirect(T.ulist16[:, 0:16]), [("us", 0, 128, 1), ("ulist16", 0, 16, 1)]))
    iota(A("jj"), [[0, K24], [1, 16]], 0, small=True)
    iota(A("nat"), [[1, C]], 0, small=True)
    send_children(1)
    op("g", lambda: g.affine_select(T.eye[:], T.one[:], [[-1, 128]], OP.is_equal, 0.0, 0, 1), [A("eye")], [A("one")])

    def signs(x, h):
        lo, hi = HC * h, HC * (h + 1)
        quant(A("xq", lo, hi), A("xs", lo, hi), A(x, 4 * lo, 4 * hi))
        mm("ps%d" % (5 - h), "uq2", "us2", 0, "xq", "xs", lo, hi)
        if h == 0:
            mm("ps6", "uq2", "us2", 128, "xq", "xs", lo, hi)
        ts(A("b", lo, hi), A("ps%d" % (5 - h), 0, HC), 0.0, OP.is_gt)

    act(A("rst"), A("jj"), AF.Sign)
    lists_of(0, True)
    signs("x0", 1)

    def select(s, raw, L):
        def B(i, n=1):
            return A("sm" + s, K24 * i, K24 * (i + n))
        tt(B(0), raw, raw, OP.mult)
        for i, least in enumerate((2.3, 6.2, 12.2)):
            ts(B(1 + i), B(0), A("fac", 1, 2), OP.mult, least, OP.is_gt)
        tt(B(4, 3), B(1, 3), A("pr"), OP.mult)
        tt(B(7), B(4), B(5), OP.add)
        tt(B(8), B(6), A(L, 0, K24), OP.add)
        tt(A("d" + s), B(7), B(8), OP.add)

    for r in range(1, ROUNDS + 1):
        x, xn = "x%d" % (r - 1), "x%d" % r
        lu, L, Ln = "lu%d" % (r - 1), "lk%d" % (r - 1), "lk%d" % r
        fl = (lu, 0, K24)
        fk = (lu, K24, 2 * K24)

        signs(x, 0)
        pairs_of(r - 1)
        for h in (0, 1):
            for t in range(4):
                act(A("pp", 4 * HC * h + t, 4 * HC * (h + 1), 4), IND(x, "la%d" % t, K12 * h, K12 * (h + 1)))
            load("g", A("pp", 4 * HC * h, 4 * HC * (h + 1)), A(x, 4 * HC * h, 4 * HC * (h + 1)), "pa%d_%d" % (r, h), accum_op=OP.add)
        act(A("ga", 0, HC), IND("b", lu, 0, K12), AF.Identity, scale=-3.0, bias=3.0)
        ts(A("ga", HC, C), IND("b", lu, K12, K24), -3.0, OP.mult, 3.0, OP.add)
        tt(A("tx", HC, C), IND("b", lu, K24 + K12, 2 * K24), A("ga", HC, C), OP.add)
        tt(A("tx", 0, HC), IND("b", lu, K24, K24 + K12), A("ga", 0, HC), OP.add)
        act(A("c3"), A("tx", 0, C), AF.Relu, scale=-3.0, bias=3.0)
        ts(A("c0"), A("tx", 0, C), 0.0, OP.is_equal)
        tt(A("yy"), IND("c0", *fk), A("tx", 0, C), OP.subtract)
        tt(A("tx", C, 2 * C), IND("c3", *fl), A("yy"), OP.add)
        ts(A("c1"), A("tx", C, 2 * C), 0.0, OP.is_equal)
        act(A("gb"), IND("c1", *fl), AF.Copy, scale=3.0)
        tt(A("xx"), IND("c1", *fk), A("gb"), OP.add)
        if r == 1:
            for b in range(4):
                act(A("et", 512 * b + b, 512 * (b + 1), 4), A("eye"))
            quant(A("eq"), A("es"), A("et"))
        act(A("ts"), A("ps6", 0, HC), AF.Sign, scale=-1.0)
        scan(A("raw0"), A("wgt"), A("tx", 0, C))
        select("0", A("raw0", *VIEW24), L)
        act(A("dn"), IND("nat", "d0", 0, K24))
        scan(A("raw1"), A("wgt"), A("tx", C, 2 * C))
        select("1", A("raw1", *VIEW24), L)
        act(A("qn"), IND("dn", "d1", 0, K24))
        scan(A("raw2"), A("wgt"), A("xx"))
        tt(A("xd"), A("raw2", *VIEW24), A("raw0", *VIEW24), OP.subtract)
        select("2", A("xd"), L)
        tt(A("om"), IND("qn", "d2", 0, K24), A("sel"), OP.mult)
        act(A("on"), IND("qn", "d2", 0, K24))
        scan(A("ow"), A("rst"), A("om"))
        for t in (2, 3, 0, 1):
            ts(A("of%d" % t), A("ow", *VIEW24), 4.0, OP.mult, float(t), OP.add)
        for h in (0, 1):
            boost[0] = BOOST[h]
            for t in range(4):
                z, p = A("zt", 4 * HC * h + t, 4 * HC * (h + 1), 4), IND("pp", "of%d" % t, K12 * h, K12 * (h + 1))
                if t < 2 - h:
                    ts(z, p, 0.5, OP.mult)
                else:
                    act(z, p, AF.Copy, scale=0.5)
            quant(A("zq", HC * h, HC * (h + 1)), A("zs", HC * h, HC * (h + 1)), A("zt", 4 * HC * h, 4 * HC * (h + 1)))
            for b in range(4):
                mm("ps%d" % (4 * h + b), "wq", "wp", 128 * b, "zq", "zs", HC * h, HC * (h + 1))
        boost[0] = 0.0
        tt(A("mn"), IND("on", "kin%d" % r, 0, K24), A("sel"), OP.mult)
        scan(A("mw"), A("rst"), A("mn"))
        vcopy(A("mu"), A("mw", *VIEW24))
        send(A("min%d" % r), A("mu", K12, K24), partner(r), "rm%d" % r, "lm%d" % r, 2.0)
        for b in range(4):
            act(A("h%d" % b, 0, HC), A("ps%d" % b, 0, HC), scale=0.03125)
        for b in (0, 2):
            ts(A("h%d" % b, HC, C), A("ps%d" % (4 + b), 0, HC), 0.03125, OP.mult)
            act(A("h%d" % (b + 1), HC, C), A("ps%d" % (5 + b), 0, HC), scale=0.03125)
            vcopy(A("ht", b, 4 * HC, 4), IND("h%d" % b, "mu", 0, K12))
            act(A("ht", b + 1, 4 * HC, 4), IND("h%d" % (b + 1), "mu", 0, K12))
        quant(A("hq"), A("hs"), A("ht"))
        send(U8("dq%d" % r, 0, HC), U8("hq", 0, HC), partner(r), "rc%d" % r, "lc%d" % r, 3.0)
        send(A("ds%d" % r), A("hs"), partner(r), "rs%d" % r, "ls%d" % r, 2.7)
        for b in range(4):
            tt(A(xn, 4 * HC + b, 8 * HC, 4), IND("h%d" % b, "min%d" % r, 0, K12), A(x, 4 * HC + b, 8 * HC, 4), OP.add)
        if r < ROUNDS:
            signs(xn, 1)
        else:
            quant(A("xq", HC, C), A("xs", HC, C), A(xn, 4 * HC, 8 * HC))
        scan(A("tw"), A("wgt", 0, HC), A("ts"))
        for i in range(2):
            ts(A("tt", K12 * i, K12 * (i + 1)), A("tw", *VIEW12), A("fac", 0, 1), OP.mult, 0.5, OP.is_gt)
        tt(A("ud"), A("tt"), A("dif"), OP.mult)
        tt(A(Ln, 0, K24), A(L, 0, K24), A("ud"), OP.add)
        tt(A(Ln, 3 * K12, 4 * K12), A(L, 3 * K12, 4 * K12), A("ud", 0, K12), OP.subtract)
        tt(A(Ln, 2 * K12, 3 * K12), A(L, 2 * K12, 3 * K12), A("ud", K12, K24), OP.subtract)
        if r < ROUNDS:
            lists_of(r, False)
            send_children(r + 1)
        else:
            quant(A("vq"), A("vs"), A("vt"))
            mm("ps4", "vq", "vs", 0, "xq", "xs", HC, C)
            act(A("yo", HC, C), A("ps4", 0, HC))
            vcopy(A("lu%d" % r), A(Ln))
            act(A("lro"), IND("nat", "lu%d" % r, 0, 2 * K24))
            load("y", X(T.oc[:, 4 * HC:4 * C]), U8("xq", HC, C), "o0")
            for k in range(4):
                load("y", X(T.osc[4 * k:4 * k + 4, HC:C]), (T.xs[32 * k:32 * k + 4, HC:C], [("xs", HC, C, 1)]), "o%d" % (1 + k))
            load("y", X(T.y[:, HC:C]), A("yo", HC, C), "o5")
            for k in range(8):
                load("y", X(T.lr[k:k + 1, :]), (T.lro[16 * k:16 * k + 1, :], [("lro", 0, 2 * C, 1)]), "o%d" % (6 + k))
        for b in range(4):
            mm("ps%d" % b, "eq", "es", 128 * b, "dq%d" % r, "ds%d" % r, 0, HC)
            tt(A(xn, b, 4 * HC, 4), A("ps%d" % b, 0, HC), A(x, b, 4 * HC, 4), OP.add)

    quant(A("xq", 0, HC), A("xs", 0, HC), A("x3", 0, 4 * HC))
    mm("ps5", "vq", "vs", 0, "xq", "xs", 0, HC)
    load("s", X(T.oc[:, 0:4 * HC]), U8("xq", 0, HC), "o14")
    for k in range(4):
        load("y" if k < 2 else "s", X(T.osc[4 * k:4 * k + 4, 0:HC]), (T.xs[32 * k:32 * k + 4, 0:HC], [("xs", 0, HC, 1)]), "o%d" % (15 + k))
    vcopy(A("yo", 0, HC), A("ps5", 0, HC))
    load("y", X(T.y[:, 0:HC]), A("yo", 0, HC), "o19")
    issue(plan())
